import numpy as np
import ml_dtypes


def mxq(x, axis, fmt="e4m3"):
    dtype, down = {"e4m3": (ml_dtypes.float8_e4m3fn, 7), "e5m2": (ml_dtypes.float8_e5m2, 14)}[fmt]
    v = np.moveaxis(np.asarray(x, np.float32).astype(ml_dtypes.bfloat16).astype(np.float64), axis, -1)
    blocks = v.reshape(v.shape[:-1] + (-1, 32))
    amax = np.abs(blocks).max(-1, keepdims=True)
    byte = np.maximum(np.where(amax > 0, np.frexp(amax)[1] - 1 + 127, 0) - down, 1)
    scale = np.exp2(byte - 127.0)
    codes = (blocks / scale).astype(np.float32).astype(dtype).astype(np.float64)
    return np.moveaxis((codes * scale).reshape(v.shape), -1, axis)


WIDE = False


def mx_kscale(k):
    if not WIDE:
        return np.ones(k)
    levels = np.array([10, -10, 5, -5, 0])
    if k % 512:
        return np.exp2(np.random.permutation(np.resize(levels, k // 32))).repeat(32)
    a = np.empty((k // 512, 16))
    for p in range(k // 512):
        a[p, :8] = np.random.permutation(np.resize(levels, 8))
        for g in range(8):
            far = levels[np.abs(levels - a[p, g]) >= 10]
            a[p, g + 8] = far[np.random.randint(len(far))]
    return np.exp2(a.ravel()).repeat(32)


def f64(x):
    return np.asarray(x).astype(np.float64)


def striped(idx):
    return np.tile(idx.reshape(-1, 16).T, (8, 1)).astype(np.uint16)


def unstriped(offs):
    return offs[:16].T.reshape(-1).astype(np.int64)


E2M1 = np.array([0.0, 0.5, 1.0, 1.5, 2.0, 3.0, 4.0, 6.0, -0.0, -0.5, -1.0, -1.5, -2.0, -3.0, -4.0, -6.0])


def pack_fp4(w):
    k, n = w.shape
    w = f64(np.asarray(w, np.float32).astype(ml_dtypes.bfloat16)).reshape(k // 32, 32, n)
    amax = np.abs(w).max(1)
    mant, ex = np.frexp(amax / 6.0)
    byte = np.clip(np.where(amax > 0, np.where(mant > 0.5, ex, ex - 1) + 127, 1), 1, 254)
    scaled = (w * np.exp2(127.0 - byte)[:, None, :]).reshape(k, n).astype(np.float32)
    c = np.ascontiguousarray(scaled.reshape(k // 512, 128, 4, n).transpose(0, 1, 3, 2)).astype(ml_dtypes.float4_e2m1fn).view(np.uint8) & 0xF
    words = (c[..., 0::2] | (c[..., 1::2] << 4)).reshape(k // 512, 128, 2 * n)
    return np.ascontiguousarray(words), np.ascontiguousarray(byte.astype(np.uint8).reshape(k // 512, 16, n))


def unpack_fp4(words, scales):
    g, _, n = scales.shape
    words = np.ascontiguousarray(words).reshape(g, 128, n, 2)
    nib = np.empty((g, 128, n, 4), np.uint8)
    nib[..., 0::2] = words & 0xF
    nib[..., 1::2] = words >> 4
    vals = E2M1[nib] * np.repeat(np.exp2(scales.astype(np.float64) - 127.0), 8, axis=1)[..., None]
    return vals.transpose(0, 1, 3, 2).reshape(g * 512, n)


K, T, S, V, H, N = 512, 4096, 1024, 512, 512, 256


def setup_inputs():
    n = np.random.standard_normal
    s = mx_kscale(K)[:, None]
    u = mx_kscale(H)
    packed_w2 = pack_fp4(n((H, N)) / np.sqrt(3 * H) / u[:, None])
    packed_w3 = pack_fp4(n((H, N)) / np.sqrt(3 * H) / u[:, None])
    packed_w4 = pack_fp4(n((H, N)) / np.sqrt(3 * H) / u[:, None])
    return {
        "xT": (n((K, T)) * s).astype(np.float32),
        "w1": (n((K, H)) / np.sqrt(K) / s * u).astype(np.float32),
        "w2_words": packed_w2[0],
        "w2_scales": packed_w2[1],
        "w3_words": packed_w3[0],
        "w3_scales": packed_w3[1],
        "w4_words": packed_w4[0],
        "w4_scales": packed_w4[1],
        "offs": striped(np.random.permutation(T)[:S]),
        "pos1": striped(np.random.permutation(S)[:V]),
        "pos2": striped(np.random.permutation(S)[:V]),
        "pos3": striped(np.random.permutation(S)[:V]),
        "pos4": striped(np.random.permutation(S)[:V]),
    }


def reference(xT, w1, w2_words, w2_scales, w3_words, w3_scales, w4_words, w4_scales, offs, pos1, pos2, pos3, pos4):
    xq = mxq(f64(xT)[:, unstriped(offs)], 0, "e4m3")
    h = mxq(f64(w1), 0, "e4m3").T @ xq
    g0 = h[:, unstriped(pos1)]
    g1 = h[:, unstriped(pos2)]
    g2 = h[:, unstriped(pos3)]
    g3 = h[:, unstriped(pos4)]
    z1 = (g0 + g1 + g2 + g3) / 4
    z2 = np.maximum(np.maximum(np.maximum(g0, g1), g2), g3)
    z3 = np.minimum(np.minimum(np.minimum(g0, g1), g2), g3)
    return unpack_fp4(w2_words, w2_scales).T @ mxq(z1, 0, "e4m3") + unpack_fp4(w3_words, w3_scales).T @ mxq(z2, 0, "e4m3") + unpack_fp4(w4_words, w4_scales).T @ mxq(z3, 0, "e4m3")

@@ -1,0 +1,201 @@
+from contextlib import ExitStack
+
+import concourse.mybir as mybir
+from concourse.masks import make_identity
+
+K, T, S, V, H, N = 512, 4096, 1024, 512, 512, 256
+FLOPS = 2 * K * H * S + 3 * 2 * H * N * V
+
+F32 = mybir.dt.float32
+BF16 = mybir.dt.bfloat16
+I32 = mybir.dt.int32
+U32 = mybir.dt.uint32
+U16 = mybir.dt.uint16
+U8 = mybir.dt.uint8
+FP8X4 = mybir.dt.float8_e4m3fn_x4
+FP4X4 = mybir.dt.float4_e2m1fn_x4
+COPY = mybir.ActivationFunctionType.Copy
+MAX = mybir.AluOpType.max
+MIN = mybir.AluOpType.min
+
+P = 128
+PACK = 4
+D = 4
+PIECE = 512
+HALF = V // 2
+
+
+def tile_picked_pna_none_e_kernel(
+    tc, xT, w1, w2_words, w2_scales, w3_words, w3_scales, w4_words, w4_scales, offs, pos1, pos2, pos3, pos4, out
+):
+    nc = tc.nc
+    with ExitStack() as ctx:
+        keep = ctx.enter_context(tc.tile_pool(name="keep", bufs=1))
+        psum = ctx.enter_context(tc.psum_pool(name="psum", bufs=1))
+
+        def sbuf(shape, dtype, name):
+            return keep.tile(shape, dtype, name=name, align_bytes=64)
+
+        def bank(b, shape):
+            return psum.tile(shape, F32, name="bank%d" % b)
+
+        def quantize(values, width, name):
+            codes = sbuf([P, width], U32, name + "_codes")
+            scales = sbuf([P, width], U8, name + "_scales")
+            nc.vector.quantize_mx(out=codes[:].bitcast(FP8X4), scales=scales[:], in_=values)
+            return codes, scales
+
+        x_rows = xT.rearrange("(p j) t -> p j t", j=PACK)
+        planes = [sbuf([P, T], F32, "plane%d" % j) for j in range(PACK)]
+        offs_t = keep.tile([P, S // 16], U16, name="offs")
+        nc.sync.dma_start(out=planes[0][:], in_=x_rows[:, 0, :])
+        nc.sync.dma_start(offs_t[:], offs)
+        for j in range(1, PACK):
+            nc.sync.dma_start(out=planes[j][:], in_=x_rows[:, j, :])
+        w1_raw = sbuf([P, PACK, H], F32, "w1_raw")
+        nc.sync.dma_start(out=w1_raw[:], in_=w1.rearrange("(p j) c -> p j c", j=PACK))
+        pos_t = []
+        for d, pos in enumerate((pos1, pos2, pos3, pos4)):
+            tile = keep.tile([P, V // 16], U16, name="pos%d" % d)
+            nc.sync.dma_start(tile[:], pos)
+            pos_t.append(tile)
+        out_scales = sbuf([P, 3 * N], U8, "out_scales")
+        nc.gpsimd.memset(out_scales[:].bitcast(I32), 0)
+        out_words = []
+        for a, words in enumerate((w2_words, w3_words, w4_words)):
+            tile = sbuf([P, 2 * N], U8, "out_words%d" % a)
+            nc.sync.dma_start(out=tile[:].bitcast(I32), in_=words[0].bitcast(I32))
+            out_words.append(tile)
+        for a, scales in enumerate((w2_scales, w3_scales, w4_scales)):
+            for q in range(4):
+                nc.sync.dma_start(
+                    out=out_scales[32 * q : 32 * q + 4, a * N : (a + 1) * N].bitcast(I32),
+                    in_=scales[0, 4 * q : 4 * q + 4, :].bitcast(I32),
+                )
+        identity = sbuf([P, P], F32, "identity")
+        make_identity(nc, identity[:])
+
+        picked = [sbuf([P, PIECE, PACK], BF16, "picked%d" % s) for s in range(S // PIECE)]
+        for j in range(PACK):
+            for s in range(S // PIECE):
+                cols = slice(s * PIECE // 16, (s + 1) * PIECE // 16)
+                nc.vector.tensor_copy(picked[s][:, :, j], planes[j][:].indirect(offs_t[:, cols]))
+
+        w1_cols = w1_raw[:].rearrange("p j (m t) -> p m j t", t=PACK)
+        w1_grouped = []
+        for u in range(2):
+            tile = sbuf([P, 2, P, PACK], BF16, "w1_grouped%d" % u)
+            nc.scalar.activation(tile[:].rearrange("p t m j -> p m j t"), w1_cols[:, :, :, 2 * u : 2 * u + 2], COPY)
+            w1_grouped.append(tile)
+
+        x_q = [None, None]
+        w1_q = [None, None]
+        x_q[0] = quantize(picked[0][:].rearrange("p n j -> p (n j)"), PIECE, "x0")
+        w1_q[0] = quantize(w1_grouped[0][:].rearrange("p t m j -> p (t m j)"), 2 * P, "w1_0")
+        x_q[1] = quantize(picked[1][:].rearrange("p n j -> p (n j)"), PIECE, "x1")
+        w1_q[1] = quantize(w1_grouped[1][:].rearrange("p t m j -> p (t m j)"), 2 * P, "w1_1")
+
+        h = []
+        for t in range(PACK):
+            row = sbuf([P, S], F32, "h%d" % t)
+            w_codes, w_scales = w1_q[t // 2]
+            cols = slice((t % 2) * P, (t % 2 + 1) * P)
+            for s in range(S // PIECE):
+                acc = bank(4 + (2 * t + s) % 4, [P, PIECE])
+                nc.tensor.matmul_mx(
+                    out=acc[:],
+                    lhsT=w_codes[:, cols].bitcast(FP8X4),
+                    lhsT_scale=w_scales[:, cols],
+                    rhs=x_q[s][0][:].bitcast(FP8X4),
+                    rhs_scale=x_q[s][1][:],
+                    start=True,
+                    stop=True,
+                )
+                nc.scalar.copy(row[:, s * PIECE : (s + 1) * PIECE], acc[:])
+            h.append(row)
+
+        sums = [bank(b, [P, PACK * P]) for b in range(V // P)]
+        rounded = [[None, None] for d in range(D)]
+
+        def round_neighbours(d, half):
+            tile = sbuf([P, HALF * PACK], BF16, "rounded%d_%d" % (d, half))
+            source = fetched[d][:, :, half * HALF : (half + 1) * HALF]
+            nc.scalar.copy(
+                tile[:].rearrange("p (c i t) -> p c t i", i=4, t=PACK),
+                source.rearrange("p t (c i) -> p c t i", i=4),
+            )
+            rounded[d][half] = tile
+
+        fetched = []
+        for d in range(D):
+            tile = sbuf([P, PACK, V], F32, "fetched%d" % d)
+            fetched.append(tile)
+            for t in range(PACK):
+                nc.vector.tensor_copy(tile[:, t, :], h[t][:].indirect(pos_t[d][:]))
+                for b in range(V // P):
+                    nc.tensor.matmul(
+                        sums[b][:, t * P : (t + 1) * P],
+                        tile[:, t, b * P : (b + 1) * P],
+                        identity[:],
+                        start=(d == 0 and t == 0),
+                        stop=(d == D - 1 and t == PACK - 1),
+                        is_transpose=True,
+                    )
+            if d < D - 1:
+                for half in range(2):
+                    round_neighbours(d, half)
+
+        back_bank = (4, 1)
+        out_banks = ((5, 6, 7, 0), (2, 3, 4, 5))
+        for half in range(2):
+            round_neighbours(D - 1, half)
+            back = bank(back_bank[half], [P, 2, 2, P])
+            for i in range(2):
+                b = 2 * half + i
+                mean_t = sbuf([P, 2, P, 2], BF16, "mean_t%d" % b)
+                nc.scalar.activation(mean_t[:], sums[b][:].rearrange("v (u e p) -> v u p e", u=2, e=2), COPY, scale=0.25)
+                words = mean_t[:].rearrange("v u p e -> v (u p e)").bitcast(F32)
+                for u in range(2):
+                    nc.tensor.transpose(back[:, i, u, :], words[:, u * P : (u + 1) * P], identity[:])
+            mean = sbuf([P, HALF * PACK], BF16, "mean%d" % half)
+            nc.scalar.copy(
+                mean[:].bitcast(F32).rearrange("p (i v u) -> p i v u", i=2, u=2),
+                back[:].rearrange("p i u v -> p i v u"),
+            )
+
+            largest = rounded[0][half]
+            smallest = rounded[0][half]
+            for d in range(1, D):
+                nxt = sbuf([P, HALF * PACK], BF16, "largest%d_%d" % (d, half))
+                nc.vector.tensor_tensor(nxt[:], largest[:], rounded[d][half][:], MAX)
+                largest = nxt
+                nxt = sbuf([P, HALF * PACK], BF16, "smallest%d_%d" % (d, half))
+                nc.vector.tensor_tensor(nxt[:], smallest[:], rounded[d][half][:], MIN)
+                smallest = nxt
+            z_q = [None, None, None]
+            z_q[1] = quantize(largest[:], HALF, "largest%d" % half)
+            z_q[2] = quantize(smallest[:], HALF, "smallest%d" % half)
+            z_q[0] = quantize(mean[:], HALF, "mean%d" % half)
+
+            accs = [bank(b, [P, P]) for b in out_banks[half]]
+            for step, a in enumerate((1, 2, 0)):
+                for m in range(N // P):
+                    for i in range(2):
+                        cols = slice(i * P, (i + 1) * P)
+                        nc.tensor.matmul_mx(
+                            out=accs[2 * m + i][:],
+                            lhsT=out_words[a][:, 2 * P * m : 2 * P * (m + 1)].bitcast(FP4X4),
+                            lhsT_scale=out_scales[:, a * N + m * P : a * N + (m + 1) * P],
+                            rhs=z_q[a][0][:, cols].bitcast(FP8X4),
+                            rhs_scale=z_q[a][1][:, cols],
+                            start=(step == 0),
+                            stop=(step == 2),
+                        )
+            for m in range(N // P):
+                result = sbuf([P, HALF], F32, "result%d_%d" % (half, m))
+                for i in range(2):
+                    if half == 1 and m == 1:
+                        nc.vector.tensor_copy(result[:, i * P : (i + 1) * P], accs[2 * m + i][:])
+                    else:
+                        nc.scalar.copy(result[:, i * P : (i + 1) * P], accs[2 * m + i][:])
+                nc.sync.dma_start(out=out[m * P : (m + 1) * P, half * HALF : (half + 1) * HALF], in_=result[:])

@@ -111,44 +111,56 @@ def tile_picked_pna_none_e_kernel(
                     start=True,
                     stop=True,
                 )
-                nc.scalar.copy(row[:, s * PIECE : (s + 1) * PIECE], acc[:])
+                if t == 0 and s == 1:
+                    nc.vector.tensor_copy(row[:, s * PIECE : (s + 1) * PIECE], acc[:])
+                else:
+                    nc.scalar.copy(row[:, s * PIECE : (s + 1) * PIECE], acc[:])
             h.append(row)
 
         sums = [bank(b, [P, PACK * P]) for b in range(V // P)]
-        rounded = [[None, None] for d in range(D)]
+        fetched = [sbuf([P, PACK, V], F32, "fetched%d" % d) for d in range(D)]
+        rounded = [sbuf([P, V * PACK], BF16, "rounded%d" % d) for d in range(D - 1)]
+        order = [(d, t) for t in range(PACK) for d in range(D - 1)] + [(D - 1, t) for t in range(PACK)]
+        for d, t in order:
+            nc.vector.tensor_copy(fetched[d][:, t, :], h[t][:].indirect(pos_t[d][:]))
+            for b in range(V // P):
+                nc.tensor.matmul(
+                    sums[b][:, t * P : (t + 1) * P],
+                    fetched[d][:, t, b * P : (b + 1) * P],
+                    identity[:],
+                    start=((d, t) == order[0]),
+                    stop=((d, t) == order[-1]),
+                    is_transpose=True,
+                )
+            if d < D - 1 and t % 2 == 1:
+                u = t // 2
+                nc.scalar.copy(
+                    rounded[d][:].rearrange("p (c i t) -> p c t i", i=4, t=PACK)[:, :, 2 * u : 2 * u + 2, :],
+                    fetched[d][:, 2 * u : 2 * u + 2, :].rearrange("p t (c i) -> p c t i", i=4),
+                )
 
-        def round_neighbours(d, half):
-            tile = sbuf([P, HALF * PACK], BF16, "rounded%d_%d" % (d, half))
-            source = fetched[d][:, :, half * HALF : (half + 1) * HALF]
+        rounded_last = []
+        for half in range(2):
+            tile = sbuf([P, HALF * PACK], BF16, "rounded_last%d" % half)
             nc.scalar.copy(
                 tile[:].rearrange("p (c i t) -> p c t i", i=4, t=PACK),
-                source.rearrange("p t (c i) -> p c t i", i=4),
+                fetched[D - 1][:, :, half * HALF : (half + 1) * HALF].rearrange("p t (c i) -> p c t i", i=4),
             )
-            rounded[d][half] = tile
+            rounded_last.append(tile)
 
-        fetched = []
-        for d in range(D):
-            tile = sbuf([P, PACK, V], F32, "fetched%d" % d)
-            fetched.append(tile)
-            for t in range(PACK):
-                nc.vector.tensor_copy(tile[:, t, :], h[t][:].indirect(pos_t[d][:]))
-                for b in range(V // P):
-                    nc.tensor.matmul(
-                        sums[b][:, t * P : (t + 1) * P],
-                        tile[:, t, b * P : (b + 1) * P],
-                        identity[:],
-                        start=(d == 0 and t == 0),
-                        stop=(d == D - 1 and t == PACK - 1),
-                        is_transpose=True,
-                    )
-            if d < D - 1:
-                for half in range(2):
-                    round_neighbours(d, half)
+        largest_before = rounded[0]
+        smallest_before = rounded[0]
+        for d in range(1, D - 1):
+            nxt = sbuf([P, V * PACK], BF16, "largest%d" % d)
+            nc.vector.tensor_tensor(nxt[:], largest_before[:], rounded[d][:], MAX)
+            largest_before = nxt
+            nxt = sbuf([P, V * PACK], BF16, "smallest%d" % d)
+            nc.vector.tensor_tensor(nxt[:], smallest_before[:], rounded[d][:], MIN)
+            smallest_before = nxt
 
         back_bank = (4, 1)
         out_banks = ((5, 6, 7, 0), (2, 3, 4, 5))
         for half in range(2):
-            round_neighbours(D - 1, half)
             back = bank(back_bank[half], [P, 2, 2, P])
             for i in range(2):
                 b = 2 * half + i
@@ -163,15 +175,11 @@ def tile_picked_pna_none_e_kernel(
                 back[:].rearrange("p i u v -> p i v u"),
             )
 
-            largest = rounded[0][half]
-            smallest = rounded[0][half]
-            for d in range(1, D):
-                nxt = sbuf([P, HALF * PACK], BF16, "largest%d_%d" % (d, half))
-                nc.vector.tensor_tensor(nxt[:], largest[:], rounded[d][half][:], MAX)
-                largest = nxt
-                nxt = sbuf([P, HALF * PACK], BF16, "smallest%d_%d" % (d, half))
-                nc.vector.tensor_tensor(nxt[:], smallest[:], rounded[d][half][:], MIN)
-                smallest = nxt
+            span = slice(half * HALF * PACK, (half + 1) * HALF * PACK)
+            largest = sbuf([P, HALF * PACK], BF16, "largest_all%d" % half)
+            nc.vector.tensor_tensor(largest[:], largest_before[:, span], rounded_last[half][:], MAX)
+            smallest = sbuf([P, HALF * PACK], BF16, "smallest_all%d" % half)
+            nc.vector.tensor_tensor(smallest[:], smallest_before[:, span], rounded_last[half][:], MIN)
             z_q = [None, None, None]
             z_q[1] = quantize(largest[:], HALF, "largest%d" % half)
             z_q[2] = quantize(smallest[:], HALF, "smallest%d" % half)

@@ -33,8 +33,8 @@ def tile_picked_pna_none_e_kernel(
         keep = ctx.enter_context(tc.tile_pool(name="keep", bufs=1))
         psum = ctx.enter_context(tc.psum_pool(name="psum", bufs=1))
 
-        def sbuf(shape, dtype, name):
-            return keep.tile(shape, dtype, name=name, align_bytes=64)
+        def sbuf(shape, dtype, name, tag=None):
+            return keep.tile(shape, dtype, name=name, tag=tag or name, align_bytes=64)
 
         def bank(b, shape):
             return psum.tile(shape, F32, name="bank%d" % b)
@@ -92,61 +92,92 @@ def tile_picked_pna_none_e_kernel(
         w1_q = [None, None]
         x_q[0] = quantize(picked[0][:].rearrange("p n j -> p (n j)"), PIECE, "x0")
         w1_q[0] = quantize(w1_grouped[0][:].rearrange("p t m j -> p (t m j)"), 2 * P, "w1_0")
-        x_q[1] = quantize(picked[1][:].rearrange("p n j -> p (n j)"), PIECE, "x1")
+        late_codes = sbuf([P, PIECE], U32, "x1_codes", tag="w1_grouped0")
+        late_scales = sbuf([P, PIECE], U8, "x1_scales")
+        for i in range(2):
+            cols = slice(i * PIECE // 2, (i + 1) * PIECE // 2)
+            nc.vector.quantize_mx(
+                out=late_codes[:, cols].bitcast(FP8X4),
+                scales=late_scales[:, cols],
+                in_=picked[1][:, cols, :].rearrange("p n j -> p (n j)"),
+            )
+        x_q[1] = (late_codes, late_scales)
         w1_q[1] = quantize(w1_grouped[1][:].rearrange("p t m j -> p (t m j)"), 2 * P, "w1_1")
 
         h = []
+        h_passes = 0
         for t in range(PACK):
             row = sbuf([P, S], F32, "h%d" % t)
             w_codes, w_scales = w1_q[t // 2]
             cols = slice((t % 2) * P, (t % 2 + 1) * P)
-            for s in range(S // PIECE):
-                acc = bank(4 + (2 * t + s) % 4, [P, PIECE])
+            spans = [(0, 0, PIECE), (1, 0, PIECE // 2), (1, PIECE // 2, PIECE)] if t == 0 else [(0, 0, PIECE), (1, 0, PIECE)]
+            for s, lo, hi in spans:
+                acc = bank((4, 5, 6, 4, 7, 5, 6, 4, 7)[h_passes], [P, hi - lo])
+                h_passes = h_passes + 1
                 nc.tensor.matmul_mx(
                     out=acc[:],
                     lhsT=w_codes[:, cols].bitcast(FP8X4),
                     lhsT_scale=w_scales[:, cols],
-                    rhs=x_q[s][0][:].bitcast(FP8X4),
-                    rhs_scale=x_q[s][1][:],
+                    rhs=x_q[s][0][:, lo:hi].bitcast(FP8X4),
+                    rhs_scale=x_q[s][1][:, lo:hi],
                     start=True,
                     stop=True,
                 )
                 if t == 0 and s == 1:
-                    nc.vector.tensor_copy(row[:, s * PIECE : (s + 1) * PIECE], acc[:])
+                    nc.vector.tensor_copy(row[:, s * PIECE + lo : s * PIECE + hi], acc[:])
                 else:
-                    nc.scalar.copy(row[:, s * PIECE : (s + 1) * PIECE], acc[:])
+                    nc.scalar.copy(row[:, s * PIECE + lo : s * PIECE + hi], acc[:])
             h.append(row)
 
-        sums = [bank(b, [P, PACK * P]) for b in range(V // P)]
-        fetched = [sbuf([P, PACK, V], F32, "fetched%d" % d) for d in range(D)]
+        blocks = V // P
+        sums = [bank(b, [P, PACK * P]) for b in range(blocks)]
+        fetched = {}
         rounded = [sbuf([P, V * PACK], BF16, "rounded%d" % d) for d in range(D - 1)]
-        order = [(d, t) for t in range(PACK) for d in range(D - 1)] + [(D - 1, t) for t in range(PACK)]
+        rounded_last = [sbuf([P, HALF * PACK], BF16, "rounded_last%d" % half) for half in range(2)]
+
+        def round_pair(target, d, u, cols):
+            nc.scalar.copy(
+                target[:].rearrange("p (c i t) -> p c t i", i=4, t=PACK)[:, :, 2 * u : 2 * u + 2, :],
+                fetched[d, u][:, :, cols].rearrange("p t (c i) -> p c t i", i=4),
+            )
+
+        order = [(d, t) for t in range(PACK) for d in range(2)]
+        order = order + [(d, 2 * u + e) for u in range(2) for d in range(2, D) for e in range(2)]
         for d, t in order:
-            nc.vector.tensor_copy(fetched[d][:, t, :], h[t][:].indirect(pos_t[d][:]))
-            for b in range(V // P):
+            if t % 2 == 0:
+                fetched[d, t // 2] = sbuf([P, 2, V], F32, "fetched%d_%d" % (d, t // 2), tag="fetched%d_%d" % (d % 2, t // 2))
+            pair = fetched[d, t // 2]
+            nc.vector.tensor_copy(pair[:, t % 2, :], h[t][:].indirect(pos_t[d][:]))
+            for b in range(blocks):
                 nc.tensor.matmul(
                     sums[b][:, t * P : (t + 1) * P],
-                    fetched[d][:, t, b * P : (b + 1) * P],
+                    pair[:, t % 2, b * P : (b + 1) * P],
                     identity[:],
                     start=((d, t) == order[0]),
                     stop=((d, t) == order[-1]),
                     is_transpose=True,
                 )
             if d < D - 1 and t % 2 == 1:
-                u = t // 2
-                nc.scalar.copy(
-                    rounded[d][:].rearrange("p (c i t) -> p c t i", i=4, t=PACK)[:, :, 2 * u : 2 * u + 2, :],
-                    fetched[d][:, 2 * u : 2 * u + 2, :].rearrange("p t (c i) -> p c t i", i=4),
-                )
+                round_pair(rounded[d], d, t // 2, slice(0, V))
+            if d == D - 1 and t == 1:
+                for half in range(2):
+                    round_pair(rounded_last[half], d, 0, slice(half * HALF, (half + 1) * HALF))
 
-        rounded_last = []
+        backs = [bank(5 + half, [P, 2, 2, P]) for half in range(2)]
+        for b in range(blocks):
+            mean_t = sbuf([P, 2, P, 2], BF16, "mean_t%d" % b)
+            nc.scalar.activation(mean_t[:], sums[b][:].rearrange("v (u e p) -> v u p e", u=2, e=2), COPY, scale=0.25)
+            words = mean_t[:].rearrange("v u p e -> v (u p e)").bitcast(F32)
+            for u in range(2):
+                nc.tensor.transpose(backs[b // 2][:, b % 2, u, :], words[:, u * P : (u + 1) * P], identity[:])
+        mean = sbuf([P, V * PACK], BF16, "mean")
         for half in range(2):
-            tile = sbuf([P, HALF * PACK], BF16, "rounded_last%d" % half)
             nc.scalar.copy(
-                tile[:].rearrange("p (c i t) -> p c t i", i=4, t=PACK),
-                fetched[D - 1][:, :, half * HALF : (half + 1) * HALF].rearrange("p t (c i) -> p c t i", i=4),
+                mean[:, half * HALF * PACK : (half + 1) * HALF * PACK].bitcast(F32).rearrange("p (i v u) -> p i v u", i=2, u=2),
+                backs[half][:].rearrange("p i u v -> p i v u"),
             )
-            rounded_last.append(tile)
+        for half in range(2):
+            round_pair(rounded_last[half], D - 1, 1, slice(half * HALF, (half + 1) * HALF))
 
         largest_before = rounded[0]
         smallest_before = rounded[0]
@@ -158,52 +189,67 @@ def tile_picked_pna_none_e_kernel(
             nc.vector.tensor_tensor(nxt[:], smallest_before[:], rounded[d][:], MIN)
             smallest_before = nxt
 
-        back_bank = (4, 1)
-        out_banks = ((5, 6, 7, 0), (2, 3, 4, 5))
-        for half in range(2):
-            back = bank(back_bank[half], [P, 2, 2, P])
-            for i in range(2):
-                b = 2 * half + i
-                mean_t = sbuf([P, 2, P, 2], BF16, "mean_t%d" % b)
-                nc.scalar.activation(mean_t[:], sums[b][:].rearrange("v (u e p) -> v u p e", u=2, e=2), COPY, scale=0.25)
-                words = mean_t[:].rearrange("v u p e -> v (u p e)").bitcast(F32)
-                for u in range(2):
-                    nc.tensor.transpose(back[:, i, u, :], words[:, u * P : (u + 1) * P], identity[:])
-            mean = sbuf([P, HALF * PACK], BF16, "mean%d" % half)
-            nc.scalar.copy(
-                mean[:].bitcast(F32).rearrange("p (i v u) -> p i v u", i=2, u=2),
-                back[:].rearrange("p i u v -> p i v u"),
-            )
+        out_banks = ((0, 4), (1, 7), (2, 5), (3, 6))
+        accs = [[bank(out_banks[b][m], [P, P]) for m in range(N // P)] for b in range(blocks)]
 
-            span = slice(half * HALF * PACK, (half + 1) * HALF * PACK)
-            largest = sbuf([P, HALF * PACK], BF16, "largest_all%d" % half)
-            nc.vector.tensor_tensor(largest[:], largest_before[:, span], rounded_last[half][:], MAX)
-            smallest = sbuf([P, HALF * PACK], BF16, "smallest_all%d" % half)
-            nc.vector.tensor_tensor(smallest[:], smallest_before[:, span], rounded_last[half][:], MIN)
-            z_q = [None, None, None]
-            z_q[1] = quantize(largest[:], HALF, "largest%d" % half)
-            z_q[2] = quantize(smallest[:], HALF, "smallest%d" % half)
-            z_q[0] = quantize(mean[:], HALF, "mean%d" % half)
-
-            accs = [bank(b, [P, P]) for b in out_banks[half]]
-            for step, a in enumerate((1, 2, 0)):
-                for m in range(N // P):
-                    for i in range(2):
-                        cols = slice(i * P, (i + 1) * P)
-                        nc.tensor.matmul_mx(
-                            out=accs[2 * m + i][:],
-                            lhsT=out_words[a][:, 2 * P * m : 2 * P * (m + 1)].bitcast(FP4X4),
-                            lhsT_scale=out_scales[:, a * N + m * P : a * N + (m + 1) * P],
-                            rhs=z_q[a][0][:, cols].bitcast(FP8X4),
-                            rhs_scale=z_q[a][1][:, cols],
-                            start=(step == 0),
-                            stop=(step == 2),
-                        )
+        def out_passes(a, b, codes, scales, first):
+            cols = slice(first, first + P)
             for m in range(N // P):
-                result = sbuf([P, HALF], F32, "result%d_%d" % (half, m))
-                for i in range(2):
-                    if half == 1 and m == 1:
-                        nc.vector.tensor_copy(result[:, i * P : (i + 1) * P], accs[2 * m + i][:])
-                    else:
-                        nc.scalar.copy(result[:, i * P : (i + 1) * P], accs[2 * m + i][:])
-                nc.sync.dma_start(out=out[m * P : (m + 1) * P, half * HALF : (half + 1) * HALF], in_=result[:])
+                nc.tensor.matmul_mx(
+                    out=accs[b][m][:],
+                    lhsT=out_words[a][:, 2 * P * m : 2 * P * (m + 1)].bitcast(FP4X4),
+                    lhsT_scale=out_scales[:, a * N + m * P : a * N + (m + 1) * P],
+                    rhs=codes[:, cols].bitcast(FP8X4),
+                    rhs_scale=scales[:, cols],
+                    start=(a == 0),
+                    stop=(a == 2),
+                )
+
+        codes, scales = quantize(mean[:], V, "mean")
+        for b in range(blocks):
+            out_passes(0, b, codes, scales, b * P)
+
+        largest = []
+        for half in range(2):
+            tile = sbuf([P, HALF * PACK], BF16, "largest_all%d" % half)
+            span = slice(half * HALF * PACK, (half + 1) * HALF * PACK)
+            nc.vector.tensor_tensor(tile[:], largest_before[:, span], rounded_last[half][:], MAX)
+            largest.append(tile)
+
+        def largest_passes(half):
+            codes, scales = quantize(largest[half][:], HALF, "largest%d" % half)
+            for i in range(2):
+                out_passes(1, 2 * half + i, codes, scales, i * P)
+
+        smallest = []
+
+        def take_smallest(b):
+            tile = sbuf([P, P * PACK], BF16, "smallest_all%d" % b)
+            nc.vector.tensor_tensor(
+                tile[:],
+                smallest_before[:, b * P * PACK : (b + 1) * P * PACK],
+                rounded_last[b // 2][:, (b % 2) * P * PACK : (b % 2 + 1) * P * PACK],
+                MIN,
+            )
+            smallest.append(tile)
+
+        out_rows = out.rearrange("(m p) v -> p m v", p=P)
+
+        def finish(b):
+            codes, scales = quantize(smallest[b][:], P, "smallest%d" % b)
+            out_passes(2, b, codes, scales, 0)
+            result = sbuf([P, N // P, P], F32, "result%d" % b)
+            nc.scalar.copy(result[:, 0, :], accs[b][0][:])
+            if b == blocks - 1:
+                nc.vector.tensor_copy(result[:, 1, :], accs[b][1][:])
+            else:
+                nc.scalar.copy(result[:, 1, :], accs[b][1][:])
+            nc.sync.dma_start(out=out_rows[:, :, b * P : (b + 1) * P], in_=result[:])
+
+        largest_passes(0)
+        take_smallest(0)
+        largest_passes(1)
+        for b in range(1, blocks):
+            take_smallest(b)
+            finish(b - 1)
+        finish(blocks - 1)

@@ -39,11 +39,17 @@ def tile_picked_pna_none_e_kernel(
         def bank(b, shape):
             return psum.tile(shape, F32, name="bank%d" % b)
 
-        def quantize(values, width, name):
-            codes = sbuf([P, width], U32, name + "_codes")
+        def quantize(values, width, name, tag=None):
+            codes = sbuf([P, width], U32, name + "_codes", tag=tag)
             scales = sbuf([P, width], U8, name + "_scales")
             nc.vector.quantize_mx(out=codes[:].bitcast(FP8X4), scales=scales[:], in_=values)
             return codes, scales
+
+        def woven(tile):
+            return tile.rearrange("p (c i t) -> p c t i", i=4, t=PACK)
+
+        def by_plane(tile):
+            return tile.rearrange("p t (c i) -> p c t i", i=4)
 
         x_rows = xT.rearrange("(p j) t -> p j t", j=PACK)
         planes = [sbuf([P, T], F32, "plane%d" % j) for j in range(PACK)]
@@ -52,8 +58,10 @@ def tile_picked_pna_none_e_kernel(
         nc.sync.dma_start(offs_t[:], offs)
         for j in range(1, PACK):
             nc.sync.dma_start(out=planes[j][:], in_=x_rows[:, j, :])
-        w1_raw = sbuf([P, PACK, H], F32, "w1_raw")
-        nc.sync.dma_start(out=w1_raw[:], in_=w1.rearrange("(p j) c -> p j c", j=PACK))
+        w1_rows = w1.rearrange("(p j) c -> p j c", j=PACK)
+        w1_raw = [sbuf([P, PACK, H // 2], F32, "w1_raw%d" % half) for half in range(2)]
+        for half in range(2):
+            nc.sync.dma_start(out=w1_raw[half][:], in_=w1_rows[:, :, half * H // 2 : (half + 1) * H // 2])
         pos_t = []
         for d, pos in enumerate((pos1, pos2, pos3, pos4)):
             tile = keep.tile([P, V // 16], U16, name="pos%d" % d)
@@ -75,22 +83,29 @@ def tile_picked_pna_none_e_kernel(
         identity = sbuf([P, P], F32, "identity")
         make_identity(nc, identity[:])
 
-        picked = [sbuf([P, PIECE, PACK], BF16, "picked%d" % s) for s in range(S // PIECE)]
+        picked = [sbuf([P, PIECE * PACK], BF16, "picked%d" % s) for s in range(S // PIECE)]
+        second = [sbuf([P, 2, PIECE], BF16, "second%d" % u) for u in range(2)]
         for j in range(PACK):
-            for s in range(S // PIECE):
-                cols = slice(s * PIECE // 16, (s + 1) * PIECE // 16)
-                nc.vector.tensor_copy(picked[s][:, :, j], planes[j][:].indirect(offs_t[:, cols]))
+            nc.vector.tensor_copy(
+                picked[0][:].rearrange("p (n j) -> p n j", j=PACK)[:, :, j], planes[j][:].indirect(offs_t[:, : PIECE // 16])
+            )
+            nc.scalar.activation(second[j // 2][:, j % 2, :], planes[j][:].indirect(offs_t[:, PIECE // 16 :]), COPY)
+            if j == 1:
+                nc.scalar.copy(woven(picked[1][:])[:, :, 0:2, :], by_plane(second[0][:]))
+        nc.vector.tensor_copy(woven(picked[1][:])[:, :, 2:4, :], by_plane(second[1][:]))
 
-        w1_cols = w1_raw[:].rearrange("p j (m t) -> p m j t", t=PACK)
-        w1_grouped = []
-        for u in range(2):
-            tile = sbuf([P, 2, P, PACK], BF16, "w1_grouped%d" % u)
-            nc.scalar.activation(tile[:].rearrange("p t m j -> p m j t"), w1_cols[:, :, :, 2 * u : 2 * u + 2], COPY)
-            w1_grouped.append(tile)
-
+        w1_grouped = [sbuf([P, 2, P, PACK], BF16, "w1_grouped%d" % u) for u in range(2)]
+        for half in range(2):
+            w1_cols = w1_raw[half][:].rearrange("p j (m t) -> p m j t", t=PACK)
+            for u in range(2):
+                nc.scalar.activation(
+                    w1_grouped[u][:, :, half * P // 2 : (half + 1) * P // 2, :].rearrange("p t m j -> p m j t"),
+                    w1_cols[:, :, :, 2 * u : 2 * u + 2],
+                    COPY,
+                )
         x_q = [None, None]
         w1_q = [None, None]
-        x_q[0] = quantize(picked[0][:].rearrange("p n j -> p (n j)"), PIECE, "x0")
+        x_q[0] = quantize(picked[0][:], PIECE, "x0")
         w1_q[0] = quantize(w1_grouped[0][:].rearrange("p t m j -> p (t m j)"), 2 * P, "w1_0")
         late_codes = sbuf([P, PIECE], U32, "x1_codes", tag="w1_grouped0")
         late_scales = sbuf([P, PIECE], U8, "x1_scales")
@@ -99,21 +114,33 @@ def tile_picked_pna_none_e_kernel(
             nc.vector.quantize_mx(
                 out=late_codes[:, cols].bitcast(FP8X4),
                 scales=late_scales[:, cols],
-                in_=picked[1][:, cols, :].rearrange("p n j -> p (n j)"),
+                in_=picked[1][:, i * PIECE * 2 : (i + 1) * PIECE * 2],
             )
         x_q[1] = (late_codes, late_scales)
-        w1_q[1] = quantize(w1_grouped[1][:].rearrange("p t m j -> p (t m j)"), 2 * P, "w1_1")
+
+        blocks = V // P
+        sums = [bank(b, [P, PACK * P]) for b in range(blocks)]
+
+        def add_turned(fetched, d, t, first, width):
+            for b in range(first // P, (first + width) // P):
+                nc.tensor.matmul(
+                    sums[b][:, t * P : (t + 1) * P],
+                    fetched[:, t, b * P - first : (b + 1) * P - first],
+                    identity[:],
+                    start=(d == 0 and t == 0),
+                    stop=(d == D - 1 and t == PACK - 1),
+                    is_transpose=True,
+                )
 
         h = []
-        h_passes = 0
+        early = [sbuf([P, PACK, V], F32, "early%d" % d) for d in range(2)]
         for t in range(PACK):
             row = sbuf([P, S], F32, "h%d" % t)
             w_codes, w_scales = w1_q[t // 2]
             cols = slice((t % 2) * P, (t % 2 + 1) * P)
             spans = [(0, 0, PIECE), (1, 0, PIECE // 2), (1, PIECE // 2, PIECE)] if t == 0 else [(0, 0, PIECE), (1, 0, PIECE)]
-            for s, lo, hi in spans:
-                acc = bank((4, 5, 6, 4, 7, 5, 6, 4, 7)[h_passes], [P, hi - lo])
-                h_passes = h_passes + 1
+            for i, (s, lo, hi) in enumerate(spans):
+                acc = bank(5 + i if t == 0 else 5 + s * (2 - t % 2), [P, hi - lo])
                 nc.tensor.matmul_mx(
                     out=acc[:],
                     lhsT=w_codes[:, cols].bitcast(FP8X4),
@@ -123,133 +150,109 @@ def tile_picked_pna_none_e_kernel(
                     start=True,
                     stop=True,
                 )
-                if t == 0 and s == 1:
+                if (s == 0) == (t > 0):
                     nc.vector.tensor_copy(row[:, s * PIECE + lo : s * PIECE + hi], acc[:])
                 else:
                     nc.scalar.copy(row[:, s * PIECE + lo : s * PIECE + hi], acc[:])
+            if t == 0:
+                w1_q[1] = quantize(w1_grouped[1][:].rearrange("p t m j -> p (t m j)"), 2 * P, "w1_1")
             h.append(row)
+            nc.scalar.activation(early[0][:, t, :], row[:].indirect(pos_t[0][:]), COPY)
+            nc.vector.tensor_copy(early[1][:, t, :], row[:].indirect(pos_t[1][:]))
+        for t in range(PACK):
+            for d in range(2):
+                add_turned(early[d], d, t, 0, V)
 
-        blocks = V // P
-        sums = [bank(b, [P, PACK * P]) for b in range(blocks)]
-        fetched = {}
-        rounded = [sbuf([P, V * PACK], BF16, "rounded%d" % d) for d in range(D - 1)]
-        rounded_last = [sbuf([P, HALF * PACK], BF16, "rounded_last%d" % half) for half in range(2)]
+        largest_early = sbuf([P, V * PACK], BF16, "largest_early")
+        smallest_early = sbuf([P, V * PACK], BF16, "smallest_early")
+        nc.vector.tensor_tensor(woven(largest_early[:]), by_plane(early[0][:]), by_plane(early[1][:]), MAX)
+        nc.vector.tensor_tensor(woven(smallest_early[:]), by_plane(early[0][:]), by_plane(early[1][:]), MIN)
 
-        def round_pair(target, d, u, cols):
-            nc.scalar.copy(
-                target[:].rearrange("p (c i t) -> p c t i", i=4, t=PACK)[:, :, 2 * u : 2 * u + 2, :],
-                fetched[d, u][:, :, cols].rearrange("p t (c i) -> p c t i", i=4),
-            )
+        out_rows = out.rearrange("(m p) v -> p m v", p=P)
+        accs = [[bank(b, [P, HALF]) for b in pair] for pair in ((6, 7), (0, 1))]
 
-        order = [(d, t) for t in range(PACK) for d in range(2)]
-        order = order + [(d, 2 * u + e) for u in range(2) for d in range(2, D) for e in range(2)]
-        for d, t in order:
-            if t % 2 == 0:
-                fetched[d, t // 2] = sbuf([P, 2, V], F32, "fetched%d_%d" % (d, t // 2), tag="fetched%d_%d" % (d % 2, t // 2))
-            pair = fetched[d, t // 2]
-            nc.vector.tensor_copy(pair[:, t % 2, :], h[t][:].indirect(pos_t[d][:]))
-            for b in range(blocks):
-                nc.tensor.matmul(
-                    sums[b][:, t * P : (t + 1) * P],
-                    pair[:, t % 2, b * P : (b + 1) * P],
-                    identity[:],
-                    start=((d, t) == order[0]),
-                    stop=((d, t) == order[-1]),
-                    is_transpose=True,
+        def fetch(tile, d, t, first, width, on_vector=False, turn=True):
+            window = h[t][:].indirect(pos_t[d][:, first // 16 : (first + width) // 16])
+            if on_vector:
+                nc.vector.tensor_copy(tile[:, t, :], window)
+            else:
+                nc.scalar.activation(tile[:, t, :], window, COPY)
+            if turn:
+                add_turned(tile, d, t, first, width)
+
+        def codes_of(a, values, first, width, tag=None):
+            return quantize(values[:], width, "z%d_%d" % (a, first), tag=tag)
+
+        def out_passes(a, quantized, first, width, start, stop):
+            codes, scales = quantized
+            for m in range(N // P):
+                nc.tensor.matmul_mx(
+                    out=accs[first // HALF][m][:, first % HALF : first % HALF + width],
+                    lhsT=out_words[a][:, 2 * P * m : 2 * P * (m + 1)].bitcast(FP4X4),
+                    lhsT_scale=out_scales[:, a * N + m * P : a * N + (m + 1) * P],
+                    rhs=codes[:].bitcast(FP8X4),
+                    rhs_scale=scales[:],
+                    start=start,
+                    stop=stop,
                 )
-            if d < D - 1 and t % 2 == 1:
-                round_pair(rounded[d], d, t // 2, slice(0, V))
-            if d == D - 1 and t == 1:
-                for half in range(2):
-                    round_pair(rounded_last[half], d, 0, slice(half * HALF, (half + 1) * HALF))
 
-        backs = [bank(5 + half, [P, 2, 2, P]) for half in range(2)]
-        for b in range(blocks):
+        def first_level(late, first):
+            hi_late, lo_late = [sbuf([P, HALF * PACK], BF16, "%s%d" % (name, first)) for name in ("hi_late", "lo_late")]
+            nc.vector.tensor_tensor(woven(hi_late[:]), by_plane(late[0][:]), by_plane(late[1][:]), MAX)
+            nc.vector.tensor_tensor(woven(lo_late[:]), by_plane(late[0][:]), by_plane(late[1][:]), MIN)
+            return hi_late, lo_late
+
+        def second_level(hi_late, lo_late, first):
+            span = slice(first * PACK, (first + HALF) * PACK)
+            hi, lo = [sbuf([P, HALF * PACK], BF16, "%s%d" % (name, first)) for name in ("hi", "lo")]
+            nc.vector.tensor_tensor(hi[:], largest_early[:, span], hi_late[:], MAX)
+            nc.vector.tensor_tensor(lo[:], smallest_early[:, span], lo_late[:], MIN)
+            return codes_of(1, hi, first, HALF), codes_of(2, lo, first, HALF)
+
+        backs = [bank(b, [P, 2, 2, P]) for b in (5, 4)]
+
+        def turn_back(b):
             mean_t = sbuf([P, 2, P, 2], BF16, "mean_t%d" % b)
             nc.scalar.activation(mean_t[:], sums[b][:].rearrange("v (u e p) -> v u p e", u=2, e=2), COPY, scale=0.25)
             words = mean_t[:].rearrange("v u p e -> v (u p e)").bitcast(F32)
             for u in range(2):
                 nc.tensor.transpose(backs[b // 2][:, b % 2, u, :], words[:, u * P : (u + 1) * P], identity[:])
-        mean = sbuf([P, V * PACK], BF16, "mean")
-        for half in range(2):
+
+        def mean_of(half):
+            mean = sbuf([P, HALF * PACK], BF16, "mean%d" % half)
             nc.scalar.copy(
-                mean[:, half * HALF * PACK : (half + 1) * HALF * PACK].bitcast(F32).rearrange("p (i v u) -> p i v u", i=2, u=2),
-                backs[half][:].rearrange("p i u v -> p i v u"),
+                mean[:].bitcast(F32).rearrange("p (i v u) -> p i v u", v=P, u=2), backs[half][:].rearrange("p i u v -> p i v u")
             )
-        for half in range(2):
-            round_pair(rounded_last[half], D - 1, 1, slice(half * HALF, (half + 1) * HALF))
+            return mean
 
-        largest_before = rounded[0]
-        smallest_before = rounded[0]
-        for d in range(1, D - 1):
-            nxt = sbuf([P, V * PACK], BF16, "largest%d" % d)
-            nc.vector.tensor_tensor(nxt[:], largest_before[:], rounded[d][:], MAX)
-            largest_before = nxt
-            nxt = sbuf([P, V * PACK], BF16, "smallest%d" % d)
-            nc.vector.tensor_tensor(nxt[:], smallest_before[:], rounded[d][:], MIN)
-            smallest_before = nxt
+        def store(half, second_engine):
+            result = sbuf([P, N // P, HALF], F32, "result%d" % half)
+            nc.scalar.copy(result[:, 0, :], accs[half][0][:])
+            second_engine(result[:, 1, :], accs[half][1][:])
+            nc.sync.dma_start(out=out_rows[:, :, half * HALF : (half + 1) * HALF], in_=result[:])
 
-        out_banks = ((0, 4), (1, 7), (2, 5), (3, 6))
-        accs = [[bank(out_banks[b][m], [P, P]) for m in range(N // P)] for b in range(blocks)]
+        late = [sbuf([P, PACK, HALF], F32, "late0_%d" % e, tag=("w1_1_codes", "w1_grouped0")[e]) for e in range(2)]
+        for t in range(PACK):
+            for e in range(2):
+                fetch(late[e], 2 + e, t, 0, HALF, on_vector=(e == 1 and t == PACK - 1))
+        first_q = second_level(*first_level(late, 0), 0)
 
-        def out_passes(a, b, codes, scales, first):
-            cols = slice(first, first + P)
-            for m in range(N // P):
-                nc.tensor.matmul_mx(
-                    out=accs[b][m][:],
-                    lhsT=out_words[a][:, 2 * P * m : 2 * P * (m + 1)].bitcast(FP4X4),
-                    lhsT_scale=out_scales[:, a * N + m * P : a * N + (m + 1) * P],
-                    rhs=codes[:, cols].bitcast(FP8X4),
-                    rhs_scale=scales[:, cols],
-                    start=(a == 0),
-                    stop=(a == 2),
-                )
-
-        codes, scales = quantize(mean[:], V, "mean")
-        for b in range(blocks):
-            out_passes(0, b, codes, scales, b * P)
-
-        largest = []
-        for half in range(2):
-            tile = sbuf([P, HALF * PACK], BF16, "largest_all%d" % half)
-            span = slice(half * HALF * PACK, (half + 1) * HALF * PACK)
-            nc.vector.tensor_tensor(tile[:], largest_before[:, span], rounded_last[half][:], MAX)
-            largest.append(tile)
-
-        def largest_passes(half):
-            codes, scales = quantize(largest[half][:], HALF, "largest%d" % half)
-            for i in range(2):
-                out_passes(1, 2 * half + i, codes, scales, i * P)
-
-        smallest = []
-
-        def take_smallest(b):
-            tile = sbuf([P, P * PACK], BF16, "smallest_all%d" % b)
-            nc.vector.tensor_tensor(
-                tile[:],
-                smallest_before[:, b * P * PACK : (b + 1) * P * PACK],
-                rounded_last[b // 2][:, (b % 2) * P * PACK : (b % 2 + 1) * P * PACK],
-                MIN,
-            )
-            smallest.append(tile)
-
-        out_rows = out.rearrange("(m p) v -> p m v", p=P)
-
-        def finish(b):
-            codes, scales = quantize(smallest[b][:], P, "smallest%d" % b)
-            out_passes(2, b, codes, scales, 0)
-            result = sbuf([P, N // P, P], F32, "result%d" % b)
-            nc.scalar.copy(result[:, 0, :], accs[b][0][:])
-            if b == blocks - 1:
-                nc.vector.tensor_copy(result[:, 1, :], accs[b][1][:])
-            else:
-                nc.scalar.copy(result[:, 1, :], accs[b][1][:])
-            nc.sync.dma_start(out=out_rows[:, :, b * P : (b + 1) * P], in_=result[:])
-
-        largest_passes(0)
-        take_smallest(0)
-        largest_passes(1)
-        for b in range(1, blocks):
-            take_smallest(b)
-            finish(b - 1)
-        finish(blocks - 1)
+        late = [sbuf([P, PACK, HALF], F32, "late1_%d" % e, tag="early%d" % e) for e in range(2)]
+        for t in range(PACK):
+            for e in range(2):
+                fetch(late[e], 2 + e, t, HALF, HALF)
+        out_passes(1, first_q[0], 0, HALF, True, False)
+        out_passes(2, first_q[1], 0, HALF, False, False)
+        turn_back(0)
+        turn_back(1)
+        second = first_level(late, HALF)
+        turn_back(2)
+        mean_q = codes_of(0, mean_of(0), 0, HALF)
+        turn_back(3)
+        out_passes(0, mean_q, 0, HALF, False, True)
+        second_q = second_level(*second, HALF)
+        out_passes(1, second_q[0], HALF, HALF, True, False)
+        out_passes(2, second_q[1], HALF, HALF, False, False)
+        out_passes(0, codes_of(0, mean_of(1), HALF, HALF), HALF, HALF, False, True)
+        store(0, nc.scalar.copy)
+        store(1, nc.vector.tensor_copy)

@@ -169,7 +169,9 @@ def tile_picked_pna_none_e_kernel(
         nc.vector.tensor_tensor(woven(smallest_early[:]), by_plane(early[0][:]), by_plane(early[1][:]), MIN)
 
         out_rows = out.rearrange("(m p) v -> p m v", p=P)
-        accs = [[bank(b, [P, HALF]) for b in pair] for pair in ((6, 7), (0, 1))]
+        accs = {0: [bank(b, [P, HALF]) for b in (6, 7)]}
+        for b in range(2):
+            accs[HALF + b * P] = [bank(2 * b + m, [P, P]) for m in range(N // P)]
 
         def fetch(tile, d, t, first, width, on_vector=False, turn=True):
             window = h[t][:].indirect(pos_t[d][:, first // 16 : (first + width) // 16])
@@ -183,15 +185,15 @@ def tile_picked_pna_none_e_kernel(
         def codes_of(a, values, first, width, tag=None):
             return quantize(values[:], width, "z%d_%d" % (a, first), tag=tag)
 
-        def out_passes(a, quantized, first, width, start, stop):
+        def out_passes(a, quantized, first, width, start, stop, skip=0):
             codes, scales = quantized
             for m in range(N // P):
                 nc.tensor.matmul_mx(
-                    out=accs[first // HALF][m][:, first % HALF : first % HALF + width],
+                    out=accs[first][m][:],
                     lhsT=out_words[a][:, 2 * P * m : 2 * P * (m + 1)].bitcast(FP4X4),
                     lhsT_scale=out_scales[:, a * N + m * P : a * N + (m + 1) * P],
-                    rhs=codes[:].bitcast(FP8X4),
-                    rhs_scale=scales[:],
+                    rhs=codes[:, skip : skip + width].bitcast(FP8X4),
+                    rhs_scale=scales[:, skip : skip + width],
                     start=start,
                     stop=stop,
                 )
@@ -225,11 +227,11 @@ def tile_picked_pna_none_e_kernel(
             )
             return mean
 
-        def store(half, second_engine):
-            result = sbuf([P, N // P, HALF], F32, "result%d" % half)
-            nc.scalar.copy(result[:, 0, :], accs[half][0][:])
-            second_engine(result[:, 1, :], accs[half][1][:])
-            nc.sync.dma_start(out=out_rows[:, :, half * HALF : (half + 1) * HALF], in_=result[:])
+        def store(first, width, second_engine):
+            result = sbuf([P, N // P, width], F32, "result%d" % first)
+            nc.scalar.copy(result[:, 0, :], accs[first][0][:])
+            second_engine(result[:, 1, :], accs[first][1][:])
+            nc.sync.dma_start(out=out_rows[:, :, first : first + width], in_=result[:])
 
         late = [sbuf([P, PACK, HALF], F32, "late0_%d" % e, tag=("w1_1_codes", "w1_grouped0")[e]) for e in range(2)]
         for t in range(PACK):
@@ -237,7 +239,7 @@ def tile_picked_pna_none_e_kernel(
                 fetch(late[e], 2 + e, t, 0, HALF, on_vector=(e == 1 and t == PACK - 1))
         first_q = second_level(*first_level(late, 0), 0)
 
-        late = [sbuf([P, PACK, HALF], F32, "late1_%d" % e, tag="early%d" % e) for e in range(2)]
+        late = [sbuf([P, PACK, HALF], F32, "late1_%d" % e, tag=("x1_scales", "w1_1_scales")[e]) for e in range(2)]
         for t in range(PACK):
             for e in range(2):
                 fetch(late[e], 2 + e, t, HALF, HALF)
@@ -250,9 +252,21 @@ def tile_picked_pna_none_e_kernel(
         mean_q = codes_of(0, mean_of(0), 0, HALF)
         turn_back(3)
         out_passes(0, mean_q, 0, HALF, False, True)
-        second_q = second_level(*second, HALF)
-        out_passes(1, second_q[0], HALF, HALF, True, False)
-        out_passes(2, second_q[1], HALF, HALF, False, False)
-        out_passes(0, codes_of(0, mean_of(1), HALF, HALF), HALF, HALF, False, True)
-        store(0, nc.scalar.copy)
-        store(1, nc.vector.tensor_copy)
+        hi = sbuf([P, HALF * PACK], BF16, "hi_last")
+        nc.vector.tensor_tensor(hi[:], largest_early[:, HALF * PACK :], second[0][:], MAX)
+        hi_q = codes_of(1, hi, HALF, HALF)
+        lows = []
+        for b in range(2):
+            out_passes(1, hi_q, HALF + b * P, P, True, False, skip=b * P)
+            lo = sbuf([P, P * PACK], BF16, "lo_last%d" % b)
+            span = slice(b * P * PACK, (b + 1) * P * PACK)
+            nc.vector.tensor_tensor(lo[:], smallest_early[:, HALF * PACK :][:, span], second[1][:, span], MIN)
+            lows.append(lo)
+        mean_q = codes_of(0, mean_of(1), HALF, HALF)
+        store(0, HALF, nc.scalar.copy)
+        for b in range(2):
+            out_passes(0, mean_q, HALF + b * P, P, False, False, skip=b * P)
+        for b in range(2):
+            out_passes(2, codes_of(2, lows[b], HALF + b * P, P), HALF + b * P, P, False, True)
+        store(HALF, P, nc.vector.tensor_copy)
+        store(HALF + P, P, nc.vector.tensor_copy)

@@ -109,17 +109,16 @@ def tile_picked_pna_none_e_kernel(
         w1_q[0] = quantize(w1_grouped[0][:].rearrange("p t m j -> p (t m j)"), 2 * P, "w1_0")
         late_codes = sbuf([P, PIECE], U32, "x1_codes", tag="w1_grouped0")
         late_scales = sbuf([P, PIECE], U8, "x1_scales")
-        for i in range(2):
-            cols = slice(i * PIECE // 2, (i + 1) * PIECE // 2)
+        cuts = (0, 256, 384, 512)
+        for lo, hi in zip(cuts, cuts[1:]):
             nc.vector.quantize_mx(
-                out=late_codes[:, cols].bitcast(FP8X4),
-                scales=late_scales[:, cols],
-                in_=picked[1][:, i * PIECE * 2 : (i + 1) * PIECE * 2],
+                out=late_codes[:, lo:hi].bitcast(FP8X4),
+                scales=late_scales[:, lo:hi],
+                in_=picked[1][:, lo * PACK : hi * PACK],
             )
         x_q[1] = (late_codes, late_scales)
 
         blocks = V // P
-        sums = [bank(b, [P, PACK * P]) for b in range(blocks)]
 
         def add_turned(fetched, d, t, first, width):
             for b in range(first // P, (first + width) // P):
@@ -138,9 +137,9 @@ def tile_picked_pna_none_e_kernel(
             row = sbuf([P, S], F32, "h%d" % t)
             w_codes, w_scales = w1_q[t // 2]
             cols = slice((t % 2) * P, (t % 2 + 1) * P)
-            spans = [(0, 0, PIECE), (1, 0, PIECE // 2), (1, PIECE // 2, PIECE)] if t == 0 else [(0, 0, PIECE), (1, 0, PIECE)]
+            spans = [(0, 0, PIECE)] + [(1, lo, hi) for lo, hi in zip(cuts, cuts[1:])] if t == 0 else [(0, 0, PIECE), (1, 0, PIECE)]
             for i, (s, lo, hi) in enumerate(spans):
-                acc = bank(5 + i if t == 0 else 5 + s * (2 - t % 2), [P, hi - lo])
+                acc = bank(((0, 1, 2, 3), (0, 4), (5, 6), (7, 1))[t][i], [P, hi - lo])
                 nc.tensor.matmul_mx(
                     out=acc[:],
                     lhsT=w_codes[:, cols].bitcast(FP8X4),
@@ -159,6 +158,7 @@ def tile_picked_pna_none_e_kernel(
             h.append(row)
             nc.scalar.activation(early[0][:, t, :], row[:].indirect(pos_t[0][:]), COPY)
             nc.vector.tensor_copy(early[1][:, t, :], row[:].indirect(pos_t[1][:]))
+        sums = [bank(b, [P, PACK * P]) for b in (2, 3, 0, 4)]
         for t in range(PACK):
             for d in range(2):
                 add_turned(early[d], d, t, 0, V)
@@ -169,9 +169,9 @@ def tile_picked_pna_none_e_kernel(
         nc.vector.tensor_tensor(woven(smallest_early[:]), by_plane(early[0][:]), by_plane(early[1][:]), MIN)
 
         out_rows = out.rearrange("(m p) v -> p m v", p=P)
-        accs = {0: [bank(b, [P, HALF]) for b in (6, 7)]}
+        accs = {0: [bank(b, [P, HALF]) for b in (7, 1)]}
         for b in range(2):
-            accs[HALF + b * P] = [bank(2 * b + m, [P, P]) for m in range(N // P)]
+            accs[HALF + b * P] = [bank(((2, 3), (0, 4))[b][m], [P, P]) for m in range(N // P)]
 
         def fetch(tile, d, t, first, width, on_vector=False, turn=True):
             window = h[t][:].indirect(pos_t[d][:, first // 16 : (first + width) // 16])
@@ -211,7 +211,7 @@ def tile_picked_pna_none_e_kernel(
             nc.vector.tensor_tensor(lo[:], smallest_early[:, span], lo_late[:], MIN)
             return codes_of(1, hi, first, HALF), codes_of(2, lo, first, HALF)
 
-        backs = [bank(b, [P, 2, 2, P]) for b in (5, 4)]
+        backs = [bank(b, [P, 2, 2, P]) for b in (5, 6)]
 
         def turn_back(b):
             mean_t = sbuf([P, 2, P, 2], BF16, "mean_t%d" % b)
@@ -249,12 +249,12 @@ def tile_picked_pna_none_e_kernel(
         turn_back(1)
         second = first_level(late, HALF)
         turn_back(2)
-        mean_q = codes_of(0, mean_of(0), 0, HALF)
+        first_mean = mean_of(0)
         turn_back(3)
-        out_passes(0, mean_q, 0, HALF, False, True)
         hi = sbuf([P, HALF * PACK], BF16, "hi_last")
         nc.vector.tensor_tensor(hi[:], largest_early[:, HALF * PACK :], second[0][:], MAX)
         hi_q = codes_of(1, hi, HALF, HALF)
+        out_passes(0, codes_of(0, first_mean, 0, HALF), 0, HALF, False, True)
         lows = []
         for b in range(2):
             out_passes(1, hi_q, HALF + b * P, P, True, False, skip=b * P)

@@ -126,7 +126,7 @@ def tile_picked_pna_none_e_kernel(
                     sums[b][:, t * P : (t + 1) * P],
                     fetched[:, t, b * P - first : (b + 1) * P - first],
                     identity[:],
-                    start=(d == 0 and t == 0),
+                    start=(d == 1 and t == 0),
                     stop=(d == D - 1 and t == PACK - 1),
                     is_transpose=True,
                 )
@@ -137,9 +137,9 @@ def tile_picked_pna_none_e_kernel(
             row = sbuf([P, S], F32, "h%d" % t)
             w_codes, w_scales = w1_q[t // 2]
             cols = slice((t % 2) * P, (t % 2 + 1) * P)
-            spans = [(0, 0, PIECE)] + [(1, lo, hi) for lo, hi in zip(cuts, cuts[1:])] if t == 0 else [(0, 0, PIECE), (1, 0, PIECE)]
+            spans = [(0, 0, PIECE)] + [(1, lo, hi) for lo, hi in zip(cuts, cuts[1:])] if t == 0 else [(1, 0, PIECE), (0, 0, PIECE)]
             for i, (s, lo, hi) in enumerate(spans):
-                acc = bank(((0, 1, 2, 3), (0, 4), (5, 6), (7, 1))[t][i], [P, hi - lo])
+                acc = bank(((0, 1, 2, 3), (4, 0), (5, 6), (7, 1))[t][i], [P, hi - lo])
                 nc.tensor.matmul_mx(
                     out=acc[:],
                     lhsT=w_codes[:, cols].bitcast(FP8X4),
@@ -149,18 +149,21 @@ def tile_picked_pna_none_e_kernel(
                     start=True,
                     stop=True,
                 )
-                if (s == 0) == (t > 0):
+                if s == 1 and t == 0:
                     nc.vector.tensor_copy(row[:, s * PIECE + lo : s * PIECE + hi], acc[:])
                 else:
                     nc.scalar.copy(row[:, s * PIECE + lo : s * PIECE + hi], acc[:])
             if t == 0:
                 w1_q[1] = quantize(w1_grouped[1][:].rearrange("p t m j -> p (t m j)"), 2 * P, "w1_1")
             h.append(row)
-            nc.scalar.activation(early[0][:, t, :], row[:].indirect(pos_t[0][:]), COPY)
             nc.vector.tensor_copy(early[1][:, t, :], row[:].indirect(pos_t[1][:]))
+            if t < 2:
+                nc.vector.tensor_copy(early[0][:, t, :], row[:].indirect(pos_t[0][:]))
+        for t in range(2, PACK):
+            nc.scalar.activation(early[0][:, t, :], h[t][:].indirect(pos_t[0][:]), COPY)
         sums = [bank(b, [P, PACK * P]) for b in (2, 3, 0, 4)]
         for t in range(PACK):
-            for d in range(2):
+            for d in (1, 0):
                 add_turned(early[d], d, t, 0, V)
 
         largest_early = sbuf([P, V * PACK], BF16, "largest_early")
@@ -242,7 +245,7 @@ def tile_picked_pna_none_e_kernel(
         late = [sbuf([P, PACK, HALF], F32, "late1_%d" % e, tag=("x1_scales", "w1_1_scales")[e]) for e in range(2)]
         for t in range(PACK):
             for e in range(2):
-                fetch(late[e], 2 + e, t, HALF, HALF)
+                fetch(late[e], 2 + e, t, HALF, HALF, on_vector=(t == PACK - 1))
         out_passes(1, first_q[0], 0, HALF, True, False)
         out_passes(2, first_q[1], 0, HALF, False, False)
         turn_back(0)

@@ -245,19 +245,22 @@ def tile_picked_pna_none_e_kernel(
         late = [sbuf([P, PACK, HALF], F32, "late1_%d" % e, tag=("x1_scales", "w1_1_scales")[e]) for e in range(2)]
         for t in range(PACK):
             for e in range(2):
-                fetch(late[e], 2 + e, t, HALF, HALF, on_vector=(t == PACK - 1))
+                fetch(late[e], 2 + e, t, HALF, HALF, on_vector=(e == 1 and t == PACK - 1))
         out_passes(1, first_q[0], 0, HALF, True, False)
         out_passes(2, first_q[1], 0, HALF, False, False)
         turn_back(0)
         turn_back(1)
-        second = first_level(late, HALF)
-        turn_back(2)
         first_mean = mean_of(0)
+        second = [sbuf([P, HALF * PACK], BF16, name) for name in ("hi_late_last", "lo_late_last")]
+        nc.vector.tensor_tensor(woven(second[0][:]), by_plane(late[0][:]), by_plane(late[1][:]), MAX)
+        out_passes(0, codes_of(0, first_mean, 0, HALF), 0, HALF, False, True)
+        nc.vector.tensor_tensor(woven(second[1][:]), by_plane(late[0][:]), by_plane(late[1][:]), MIN)
+        turn_back(2)
         turn_back(3)
+        store(0, HALF, nc.scalar.copy)
         hi = sbuf([P, HALF * PACK], BF16, "hi_last")
         nc.vector.tensor_tensor(hi[:], largest_early[:, HALF * PACK :], second[0][:], MAX)
         hi_q = codes_of(1, hi, HALF, HALF)
-        out_passes(0, codes_of(0, first_mean, 0, HALF), 0, HALF, False, True)
         lows = []
         for b in range(2):
             out_passes(1, hi_q, HALF + b * P, P, True, False, skip=b * P)
@@ -266,7 +269,6 @@ def tile_picked_pna_none_e_kernel(
             nc.vector.tensor_tensor(lo[:], smallest_early[:, HALF * PACK :][:, span], second[1][:, span], MIN)
             lows.append(lo)
         mean_q = codes_of(0, mean_of(1), HALF, HALF)
-        store(0, HALF, nc.scalar.copy)
         for b in range(2):
             out_passes(0, mean_q, HALF + b * P, P, False, False, skip=b * P)
         for b in range(2):

@@ -120,16 +120,19 @@ def tile_picked_pna_none_e_kernel(
 
         blocks = V // P
 
+        added = [[] for b in range(blocks)]
+
         def add_turned(fetched, d, t, first, width):
             for b in range(first // P, (first + width) // P):
                 nc.tensor.matmul(
                     sums[b][:, t * P : (t + 1) * P],
                     fetched[:, t, b * P - first : (b + 1) * P - first],
                     identity[:],
-                    start=(d == 1 and t == 0),
-                    stop=(d == D - 1 and t == PACK - 1),
+                    start=(len(added[b]) == 0),
+                    stop=(len(added[b]) == D * PACK - 1),
                     is_transpose=True,
                 )
+                added[b].append((d, t))
 
         h = []
         early = [sbuf([P, PACK, V], F32, "early%d" % d) for d in range(2)]
@@ -165,11 +168,6 @@ def tile_picked_pna_none_e_kernel(
         for t in range(PACK):
             for d in (1, 0):
                 add_turned(early[d], d, t, 0, V)
-
-        largest_early = sbuf([P, V * PACK], BF16, "largest_early")
-        smallest_early = sbuf([P, V * PACK], BF16, "smallest_early")
-        nc.vector.tensor_tensor(woven(largest_early[:]), by_plane(early[0][:]), by_plane(early[1][:]), MAX)
-        nc.vector.tensor_tensor(woven(smallest_early[:]), by_plane(early[0][:]), by_plane(early[1][:]), MIN)
 
         out_rows = out.rearrange("(m p) v -> p m v", p=P)
         accs = {0: [bank(b, [P, HALF]) for b in (7, 1)]}
@@ -236,39 +234,45 @@ def tile_picked_pna_none_e_kernel(
             second_engine(result[:, 1, :], accs[first][1][:])
             nc.sync.dma_start(out=out_rows[:, :, first : first + width], in_=result[:])
 
-        late = [sbuf([P, PACK, HALF], F32, "late0_%d" % e, tag=("w1_1_codes", "w1_grouped0")[e]) for e in range(2)]
-        for t in range(PACK):
-            for e in range(2):
-                fetch(late[e], 2 + e, t, 0, HALF, on_vector=(e == 1 and t == PACK - 1))
-        first_q = second_level(*first_level(late, 0), 0)
+        late_tags = (("w1_1_codes", "w1_grouped0"), ("x1_scales", "w1_1_scales"))
+        late = [[sbuf([P, PACK, HALF], F32, "late%d_%d" % (half, e), tag=late_tags[half][e]) for e in range(2)] for half in range(2)]
+        fetch(late[0][1], 3, PACK - 1, 0, HALF, on_vector=True)
+        largest_early = sbuf([P, V * PACK], BF16, "largest_early")
+        smallest_early = sbuf([P, V * PACK], BF16, "smallest_early")
+        nc.vector.tensor_tensor(woven(largest_early[:]), by_plane(early[0][:]), by_plane(early[1][:]), MAX)
+        nc.vector.tensor_tensor(woven(smallest_early[:]), by_plane(early[0][:]), by_plane(early[1][:]), MIN)
 
-        late = [sbuf([P, PACK, HALF], F32, "late1_%d" % e, tag=("x1_scales", "w1_1_scales")[e]) for e in range(2)]
-        for t in range(PACK):
-            for e in range(2):
-                fetch(late[e], 2 + e, t, HALF, HALF, on_vector=(e == 1 and t == PACK - 1))
+        for half in range(2):
+            for t in range(PACK):
+                for e in range(2):
+                    if (half, e, t) != (0, 1, PACK - 1):
+                        fetch(late[half][e], 2 + e, t, half * HALF, HALF)
+        first_q = second_level(*first_level(late[0], 0), 0)
         out_passes(1, first_q[0], 0, HALF, True, False)
         out_passes(2, first_q[1], 0, HALF, False, False)
         turn_back(0)
         turn_back(1)
         first_mean = mean_of(0)
-        second = [sbuf([P, HALF * PACK], BF16, name) for name in ("hi_late_last", "lo_late_last")]
-        nc.vector.tensor_tensor(woven(second[0][:]), by_plane(late[0][:]), by_plane(late[1][:]), MAX)
-        out_passes(0, codes_of(0, first_mean, 0, HALF), 0, HALF, False, True)
-        nc.vector.tensor_tensor(woven(second[1][:]), by_plane(late[0][:]), by_plane(late[1][:]), MIN)
         turn_back(2)
         turn_back(3)
+        last_mean = mean_of(1)
+        second = first_level(late[1], HALF)
+        out_passes(0, codes_of(0, first_mean, 0, HALF), 0, HALF, False, True)
         store(0, HALF, nc.scalar.copy)
         hi = sbuf([P, HALF * PACK], BF16, "hi_last")
         nc.vector.tensor_tensor(hi[:], largest_early[:, HALF * PACK :], second[0][:], MAX)
+        lows = [sbuf([P, P * PACK], BF16, "lo_last%d" % b) for b in range(2)]
+
+        def last_smallest(b):
+            span = slice(b * P * PACK, (b + 1) * P * PACK)
+            nc.vector.tensor_tensor(lows[b][:], smallest_early[:, HALF * PACK :][:, span], second[1][:, span], MIN)
+
+        last_smallest(0)
         hi_q = codes_of(1, hi, HALF, HALF)
-        lows = []
         for b in range(2):
             out_passes(1, hi_q, HALF + b * P, P, True, False, skip=b * P)
-            lo = sbuf([P, P * PACK], BF16, "lo_last%d" % b)
-            span = slice(b * P * PACK, (b + 1) * P * PACK)
-            nc.vector.tensor_tensor(lo[:], smallest_early[:, HALF * PACK :][:, span], second[1][:, span], MIN)
-            lows.append(lo)
-        mean_q = codes_of(0, mean_of(1), HALF, HALF)
+        last_smallest(1)
+        mean_q = codes_of(0, last_mean, HALF, HALF)
         for b in range(2):
             out_passes(0, mean_q, HALF + b * P, P, False, False, skip=b * P)
         for b in range(2):

@@ -94,6 +94,26 @@ def tile_picked_pna_none_e_kernel(
                 nc.scalar.copy(woven(picked[1][:])[:, :, 0:2, :], by_plane(second[0][:]))
         nc.vector.tensor_copy(woven(picked[1][:])[:, :, 2:4, :], by_plane(second[1][:]))
 
+        warm_codes = sbuf([P, PIECE], U32, "warm_codes")
+        warm_scales = sbuf([P, PIECE], U8, "warm_scales")
+        for i in range(2):
+            cols = slice(i * PIECE // 2, (i + 1) * PIECE // 2)
+            nc.vector.quantize_mx(
+                out=warm_codes[:, cols].bitcast(FP8X4), scales=warm_scales[:, cols], in_=second[0][:].rearrange("p e n -> p (e n)")
+            )
+        spare = bank(7, [P, PIECE])
+        nc.tensor.transpose(spare[:, :P], w1_raw[0][:, 0, :P], identity[:])
+        for i in range(3):
+            nc.tensor.matmul_mx(
+                out=spare[:],
+                lhsT=warm_codes[:, :P].bitcast(FP8X4),
+                lhsT_scale=warm_scales[:, :P],
+                rhs=warm_codes[:].bitcast(FP8X4),
+                rhs_scale=warm_scales[:],
+                start=True,
+                stop=True,
+            )
+
         w1_grouped = [sbuf([P, 2, P, PACK], BF16, "w1_grouped%d" % u) for u in range(2)]
         for half in range(2):
             w1_cols = w1_raw[half][:].rearrange("p j (m t) -> p m j t", t=PACK)

@@ -277,10 +277,10 @@ def tile_picked_pna_none_e_kernel(
         turn_back(3)
         last_mean = mean_of(1)
         second = first_level(late[1], HALF)
-        out_passes(0, codes_of(0, first_mean, 0, HALF), 0, HALF, False, True)
-        store(0, HALF, nc.scalar.copy)
         hi = sbuf([P, HALF * PACK], BF16, "hi_last")
         nc.vector.tensor_tensor(hi[:], largest_early[:, HALF * PACK :], second[0][:], MAX)
+        out_passes(0, codes_of(0, first_mean, 0, HALF), 0, HALF, False, True)
+        store(0, HALF, nc.scalar.copy)
         lows = [sbuf([P, P * PACK], BF16, "lo_last%d" % b) for b in range(2)]
 
         def last_smallest(b):

@@ -23,6 +23,7 @@ PACK = 4
 D = 4
 PIECE = 512
 HALF = V // 2
+EARLY_ON_VECTOR = 5
 
 
 def tile_picked_pna_none_e_kernel(
@@ -179,14 +180,16 @@ def tile_picked_pna_none_e_kernel(
             if t == 0:
                 w1_q[1] = quantize(w1_grouped[1][:].rearrange("p t m j -> p (t m j)"), 2 * P, "w1_1")
             h.append(row)
-            nc.vector.tensor_copy(early[1][:, t, :], row[:].indirect(pos_t[1][:]))
-            if t < 2:
-                nc.vector.tensor_copy(early[0][:, t, :], row[:].indirect(pos_t[0][:]))
-        for t in range(2, PACK):
-            nc.scalar.activation(early[0][:, t, :], h[t][:].indirect(pos_t[0][:]), COPY)
+            for d in range(2):
+                if 2 * t + d < EARLY_ON_VECTOR:
+                    nc.vector.tensor_copy(early[d][:, t, :], row[:].indirect(pos_t[d][:]))
+        for t in range(PACK):
+            for d in range(2):
+                if 2 * t + d >= EARLY_ON_VECTOR:
+                    nc.scalar.activation(early[d][:, t, :], h[t][:].indirect(pos_t[d][:]), COPY)
         sums = [bank(b, [P, PACK * P]) for b in (2, 3, 0, 4)]
         for t in range(PACK):
-            for d in (1, 0):
+            for d in range(2):
                 add_turned(early[d], d, t, 0, V)
 
         out_rows = out.rearrange("(m p) v -> p m v", p=P)
@@ -194,14 +197,13 @@ def tile_picked_pna_none_e_kernel(
         for b in range(2):
             accs[HALF + b * P] = [bank(((2, 3), (0, 4))[b][m], [P, P]) for m in range(N // P)]
 
-        def fetch(tile, d, t, first, width, on_vector=False, turn=True):
+        def fetch(tile, d, t, first, width, on_vector=False):
             window = h[t][:].indirect(pos_t[d][:, first // 16 : (first + width) // 16])
             if on_vector:
-                nc.vector.tensor_copy(tile[:, t, :], window)
+                nc.vector.tensor_copy(tile[:, t, first : first + width], window)
             else:
-                nc.scalar.activation(tile[:, t, :], window, COPY)
-            if turn:
-                add_turned(tile, d, t, first, width)
+                nc.scalar.activation(tile[:, t, first : first + width], window, COPY)
+            add_turned(tile[:, :, first : first + width], d, t, first, width)
 
         def codes_of(a, values, first, width, tag=None):
             return quantize(values[:], width, "z%d_%d" % (a, first), tag=tag)
@@ -219,18 +221,15 @@ def tile_picked_pna_none_e_kernel(
                     stop=stop,
                 )
 
-        def first_level(late, first):
-            hi_late, lo_late = [sbuf([P, HALF * PACK], BF16, "%s%d" % (name, first)) for name in ("hi_late", "lo_late")]
-            nc.vector.tensor_tensor(woven(hi_late[:]), by_plane(late[0][:]), by_plane(late[1][:]), MAX)
-            nc.vector.tensor_tensor(woven(lo_late[:]), by_plane(late[0][:]), by_plane(late[1][:]), MIN)
-            return hi_late, lo_late
+        def rounded(late, d, first):
+            tile = sbuf([P, HALF * PACK], BF16, "rounded%d_%d" % (d, first))
+            nc.vector.tensor_copy(woven(tile[:]), by_plane(late[:, :, first : first + HALF]))
+            return tile
 
-        def second_level(hi_late, lo_late, first):
-            span = slice(first * PACK, (first + HALF) * PACK)
-            hi, lo = [sbuf([P, HALF * PACK], BF16, "%s%d" % (name, first)) for name in ("hi", "lo")]
-            nc.vector.tensor_tensor(hi[:], largest_early[:, span], hi_late[:], MAX)
-            nc.vector.tensor_tensor(lo[:], smallest_early[:, span], lo_late[:], MIN)
-            return codes_of(1, hi, first, HALF), codes_of(2, lo, first, HALF)
+        def merged(name, a, b, op):
+            tile = sbuf([P, a.shape[1]], BF16, name)
+            nc.vector.tensor_tensor(tile[:], a, b, op)
+            return tile
 
         backs = [bank(b, [P, 2, 2, P]) for b in (5, 6)]
 
@@ -254,44 +253,49 @@ def tile_picked_pna_none_e_kernel(
             second_engine(result[:, 1, :], accs[first][1][:])
             nc.sync.dma_start(out=out_rows[:, :, first : first + width], in_=result[:])
 
-        late_tags = (("w1_1_codes", "w1_grouped0"), ("x1_scales", "w1_1_scales"))
-        late = [[sbuf([P, PACK, HALF], F32, "late%d_%d" % (half, e), tag=late_tags[half][e]) for e in range(2)] for half in range(2)]
-        fetch(late[0][1], 3, PACK - 1, 0, HALF, on_vector=True)
+        late = [sbuf([P, PACK, V], F32, "late%d" % e, tag=("w1_1_codes", "w1_grouped0")[e]) for e in range(2)]
+        fetch(late[0], 2, PACK - 1, 0, V, on_vector=True)
         largest_early = sbuf([P, V * PACK], BF16, "largest_early")
         smallest_early = sbuf([P, V * PACK], BF16, "smallest_early")
         nc.vector.tensor_tensor(woven(largest_early[:]), by_plane(early[0][:]), by_plane(early[1][:]), MAX)
         nc.vector.tensor_tensor(woven(smallest_early[:]), by_plane(early[0][:]), by_plane(early[1][:]), MIN)
 
+        for t in range(PACK - 1):
+            fetch(late[0], 2, t, 0, V)
+        for t in range(PACK - 1):
+            fetch(late[1], 3, t, 0, V)
         for half in range(2):
-            for t in range(PACK):
-                for e in range(2):
-                    if (half, e, t) != (0, 1, PACK - 1):
-                        fetch(late[half][e], 2 + e, t, half * HALF, HALF)
-        first_q = second_level(*first_level(late[0], 0), 0)
-        out_passes(1, first_q[0], 0, HALF, True, False)
-        out_passes(2, first_q[1], 0, HALF, False, False)
+            fetch(late[1], 3, PACK - 1, half * HALF, HALF)
+        third = [rounded(late[0], 2, half * HALF) for half in range(2)]
+        hi3, lo3 = [], []
+        for half in range(2):
+            span = slice(half * HALF * PACK, (half + 1) * HALF * PACK)
+            hi3.append(merged("hi3_%d" % half, largest_early[:, span], third[half][:], MAX))
+            lo3.append(merged("lo3_%d" % half, smallest_early[:, span], third[half][:], MIN))
+        fourth = [rounded(late[1], 3, half * HALF) for half in range(2)]
+        hi_first = merged("hi_first", hi3[0][:], fourth[0][:], MAX)
+        lo_first = merged("lo_first", lo3[0][:], fourth[0][:], MIN)
+        out_passes(1, codes_of(1, hi_first, 0, HALF), 0, HALF, True, False)
+        out_passes(2, codes_of(2, lo_first, 0, HALF), 0, HALF, False, False)
         turn_back(0)
         turn_back(1)
         first_mean = mean_of(0)
         turn_back(2)
         turn_back(3)
         last_mean = mean_of(1)
-        second = first_level(late[1], HALF)
-        hi = sbuf([P, HALF * PACK], BF16, "hi_last")
-        nc.vector.tensor_tensor(hi[:], largest_early[:, HALF * PACK :], second[0][:], MAX)
+        hi = merged("hi_last", hi3[1][:], fourth[1][:], MAX)
         out_passes(0, codes_of(0, first_mean, 0, HALF), 0, HALF, False, True)
         store(0, HALF, nc.scalar.copy)
-        lows = [sbuf([P, P * PACK], BF16, "lo_last%d" % b) for b in range(2)]
 
         def last_smallest(b):
             span = slice(b * P * PACK, (b + 1) * P * PACK)
-            nc.vector.tensor_tensor(lows[b][:], smallest_early[:, HALF * PACK :][:, span], second[1][:, span], MIN)
+            return merged("lo_last%d" % b, lo3[1][:, span], fourth[1][:, span], MIN)
 
-        last_smallest(0)
+        lows = [last_smallest(0)]
         hi_q = codes_of(1, hi, HALF, HALF)
         for b in range(2):
             out_passes(1, hi_q, HALF + b * P, P, True, False, skip=b * P)
-        last_smallest(1)
+        lows.append(last_smallest(1))
         mean_q = codes_of(0, last_mean, HALF, HALF)
         for b in range(2):
             out_passes(0, mean_q, HALF + b * P, P, False, False, skip=b * P)

@@ -17,13 +17,14 @@ FP4X4 = mybir.dt.float4_e2m1fn_x4
 COPY = mybir.ActivationFunctionType.Copy
 MAX = mybir.AluOpType.max
 MIN = mybir.AluOpType.min
+MULT = mybir.AluOpType.mult
+ADD = mybir.AluOpType.add
 
 P = 128
 PACK = 4
 D = 4
 PIECE = 512
 HALF = V // 2
-EARLY_ON_VECTOR = 5
 
 
 def tile_picked_pna_none_e_kernel(
@@ -143,20 +144,43 @@ def tile_picked_pna_none_e_kernel(
 
         added = [[] for b in range(blocks)]
 
-        def add_turned(fetched, d, t, first, width):
+        def add_turned(plane, first, width):
+            t, values = plane
             for b in range(first // P, (first + width) // P):
                 nc.tensor.matmul(
                     sums[b][:, t * P : (t + 1) * P],
-                    fetched[:, t, b * P - first : (b + 1) * P - first],
+                    values[:, b * P : (b + 1) * P],
                     identity[:],
                     start=(len(added[b]) == 0),
                     stop=(len(added[b]) == D * PACK - 1),
                     is_transpose=True,
                 )
-                added[b].append((d, t))
+                added[b].append(t)
 
         h = []
-        early = [sbuf([P, PACK, V], F32, "early%d" % d) for d in range(2)]
+        pair_tags = {(1, 0): "pair0_0", (2, 0): "w1_1_codes"}
+        pairs = {}
+
+        def plane_of(d, t):
+            if (d, t // 2) not in pairs:
+                pairs[(d, t // 2)] = sbuf([P, 2, V], F32, "pair%d_%d" % (d, t // 2), tag=pair_tags.get((d, t // 2)))
+            return t, pairs[(d, t // 2)][:, t % 2, :]
+
+        def gather(plane, d, first, width, on_vector):
+            t, values = plane
+            window = h[t][:].indirect(pos_t[d][:, first // 16 : (first + width) // 16])
+            if on_vector:
+                nc.vector.tensor_copy(values[:, first : first + width], window)
+            else:
+                nc.scalar.activation(values[:, first : first + width], window, COPY)
+
+        def paired(tile):
+            return tile.rearrange("p (c i e) -> p c e i", i=4, e=2)
+
+        def by_row(tile):
+            return tile.rearrange("p e (c i) -> p c e i", i=4)
+
+        first_list = [sbuf([P, 2 * V], BF16, "first_list%d" % u) for u in range(2)]
         for t in range(PACK):
             row = sbuf([P, S], F32, "h%d" % t)
             w_codes, w_scales = w1_q[t // 2]
@@ -180,30 +204,21 @@ def tile_picked_pna_none_e_kernel(
             if t == 0:
                 w1_q[1] = quantize(w1_grouped[1][:].rearrange("p t m j -> p (t m j)"), 2 * P, "w1_1")
             h.append(row)
-            for d in range(2):
-                if 2 * t + d < EARLY_ON_VECTOR:
-                    nc.vector.tensor_copy(early[d][:, t, :], row[:].indirect(pos_t[d][:]))
-        for t in range(PACK):
-            for d in range(2):
-                if 2 * t + d >= EARLY_ON_VECTOR:
-                    nc.scalar.activation(early[d][:, t, :], h[t][:].indirect(pos_t[d][:]), COPY)
+            gather(plane_of(0, t), 0, 0, V, True)
+            if t % 2 == 1:
+                nc.gpsimd.tensor_scalar(paired(first_list[t // 2][:]), by_row(pairs[(0, t // 2)][:]), 1.0, 0.0, MULT, ADD)
         sums = [bank(b, [P, PACK * P]) for b in (2, 3, 0, 4)]
         for t in range(PACK):
-            for d in range(2):
-                add_turned(early[d], d, t, 0, V)
+            add_turned(plane_of(0, t), 0, V)
 
         out_rows = out.rearrange("(m p) v -> p m v", p=P)
         accs = {0: [bank(b, [P, HALF]) for b in (7, 1)]}
         for b in range(2):
             accs[HALF + b * P] = [bank(((2, 3), (0, 4))[b][m], [P, P]) for m in range(N // P)]
 
-        def fetch(tile, d, t, first, width, on_vector=False):
-            window = h[t][:].indirect(pos_t[d][:, first // 16 : (first + width) // 16])
-            if on_vector:
-                nc.vector.tensor_copy(tile[:, t, first : first + width], window)
-            else:
-                nc.scalar.activation(tile[:, t, first : first + width], window, COPY)
-            add_turned(tile[:, :, first : first + width], d, t, first, width)
+        def fetch(plane, d, first, width, on_vector=False):
+            gather(plane, d, first, width, on_vector)
+            add_turned(plane, first, width)
 
         def codes_of(a, values, first, width, tag=None):
             return quantize(values[:], width, "z%d_%d" % (a, first), tag=tag)
@@ -224,11 +239,6 @@ def tile_picked_pna_none_e_kernel(
         def rounded(late, d, first):
             tile = sbuf([P, HALF * PACK], BF16, "rounded%d_%d" % (d, first))
             nc.vector.tensor_copy(woven(tile[:]), by_plane(late[:, :, first : first + HALF]))
-            return tile
-
-        def merged(name, a, b, op):
-            tile = sbuf([P, a.shape[1]], BF16, name)
-            nc.vector.tensor_tensor(tile[:], a, b, op)
             return tile
 
         backs = [bank(b, [P, 2, 2, P]) for b in (5, 6)]
@@ -253,28 +263,43 @@ def tile_picked_pna_none_e_kernel(
             second_engine(result[:, 1, :], accs[first][1][:])
             nc.sync.dma_start(out=out_rows[:, :, first : first + width], in_=result[:])
 
-        late = [sbuf([P, PACK, V], F32, "late%d" % e, tag=("w1_1_codes", "w1_grouped0")[e]) for e in range(2)]
-        fetch(late[0], 2, PACK - 1, 0, V, on_vector=True)
-        largest_early = sbuf([P, V * PACK], BF16, "largest_early")
-        smallest_early = sbuf([P, V * PACK], BF16, "smallest_early")
-        nc.vector.tensor_tensor(woven(largest_early[:]), by_plane(early[0][:]), by_plane(early[1][:]), MAX)
-        nc.vector.tensor_tensor(woven(smallest_early[:]), by_plane(early[0][:]), by_plane(early[1][:]), MIN)
+        last = sbuf([P, PACK, V], F32, "last", tag="w1_grouped0")
+        hi3 = sbuf([P, 2, 2 * V], BF16, "hi3")
+        lo3 = sbuf([P, 2, 2 * V], BF16, "lo3")
 
+        def three_lists(u):
+            hi2, lo2 = [sbuf([P, 2 * V], BF16, "%s%d" % (name, u)) for name in ("hi2_", "lo2_")]
+            nc.vector.tensor_tensor(paired(hi2[:]), by_row(pairs[(1, u)][:]), by_row(pairs[(2, u)][:]), MAX)
+            nc.vector.tensor_tensor(paired(lo2[:]), by_row(pairs[(1, u)][:]), by_row(pairs[(2, u)][:]), MIN)
+            nc.vector.tensor_tensor(hi3[:, u, :], hi2[:], first_list[u][:], MAX)
+            nc.vector.tensor_tensor(lo3[:, u, :], lo2[:], first_list[u][:], MIN)
+
+        def four_lists(name, three, first, width, op):
+            tile = sbuf([P, width * PACK], BF16, name)
+            at = first % HALF
+            nc.vector.tensor_tensor(
+                tile[:].rearrange("p (v u e) -> p v u e", u=2, e=2),
+                three[:, :, 2 * first : 2 * (first + width)].rearrange("p u (v e) -> p v u e", e=2),
+                fourth[first // HALF][:, at * PACK : (at + width) * PACK].rearrange("p (v u e) -> p v u e", u=2, e=2),
+                op,
+            )
+            return tile
+
+        fetch(plane_of(1, 3), 1, 0, V, on_vector=True)
+        for d, t in ((2, 3), (1, 2), (2, 2)):
+            fetch(plane_of(d, t), d, 0, V)
+        fetch(plane_of(1, 1), 1, 0, V, on_vector=True)
+        for d, t in ((2, 0), (1, 0), (2, 1)):
+            fetch(plane_of(d, t), d, 0, V)
+        three_lists(1)
+        three_lists(0)
+        fetch((PACK - 1, last[:, PACK - 1, :]), 3, 0, HALF, on_vector=True)
         for t in range(PACK - 1):
-            fetch(late[0], 2, t, 0, V)
-        for t in range(PACK - 1):
-            fetch(late[1], 3, t, 0, V)
-        for half in range(2):
-            fetch(late[1], 3, PACK - 1, half * HALF, HALF)
-        third = [rounded(late[0], 2, half * HALF) for half in range(2)]
-        hi3, lo3 = [], []
-        for half in range(2):
-            span = slice(half * HALF * PACK, (half + 1) * HALF * PACK)
-            hi3.append(merged("hi3_%d" % half, largest_early[:, span], third[half][:], MAX))
-            lo3.append(merged("lo3_%d" % half, smallest_early[:, span], third[half][:], MIN))
-        fourth = [rounded(late[1], 3, half * HALF) for half in range(2)]
-        hi_first = merged("hi_first", hi3[0][:], fourth[0][:], MAX)
-        lo_first = merged("lo_first", lo3[0][:], fourth[0][:], MIN)
+            fetch((t, last[:, t, :]), 3, 0, V)
+        fetch((PACK - 1, last[:, PACK - 1, :]), 3, HALF, HALF)
+        fourth = [rounded(last, 3, half * HALF) for half in range(2)]
+        hi_first = four_lists("hi_first", hi3, 0, HALF, MAX)
+        lo_first = four_lists("lo_first", lo3, 0, HALF, MIN)
         out_passes(1, codes_of(1, hi_first, 0, HALF), 0, HALF, True, False)
         out_passes(2, codes_of(2, lo_first, 0, HALF), 0, HALF, False, False)
         turn_back(0)
@@ -283,13 +308,12 @@ def tile_picked_pna_none_e_kernel(
         turn_back(2)
         turn_back(3)
         last_mean = mean_of(1)
-        hi = merged("hi_last", hi3[1][:], fourth[1][:], MAX)
+        hi = four_lists("hi_last", hi3, HALF, HALF, MAX)
         out_passes(0, codes_of(0, first_mean, 0, HALF), 0, HALF, False, True)
         store(0, HALF, nc.scalar.copy)
 
         def last_smallest(b):
-            span = slice(b * P * PACK, (b + 1) * P * PACK)
-            return merged("lo_last%d" % b, lo3[1][:, span], fourth[1][:, span], MIN)
+            return four_lists("lo_last%d" % b, lo3, HALF + b * P, P, MIN)
 
         lows = [last_smallest(0)]
         hi_q = codes_of(1, hi, HALF, HALF)

@@ -85,16 +85,18 @@ def tile_picked_pna_none_e_kernel(
         identity = sbuf([P, P], F32, "identity")
         make_identity(nc, identity[:])
 
-        picked = [sbuf([P, PIECE * PACK], BF16, "picked%d" % s) for s in range(S // PIECE)]
+        picked = sbuf([P, PIECE * PACK], BF16, "picked")
+        rest = sbuf([P, PIECE * PACK], BF16, "rest")
         second = [sbuf([P, 2, PIECE], BF16, "second%d" % u) for u in range(2)]
+
         for j in range(PACK):
             nc.vector.tensor_copy(
-                picked[0][:].rearrange("p (n j) -> p n j", j=PACK)[:, :, j], planes[j][:].indirect(offs_t[:, : PIECE // 16])
+                picked[:].rearrange("p (n j) -> p n j", j=PACK)[:, :, j], planes[j][:].indirect(offs_t[:, : PIECE // 16])
             )
             nc.scalar.activation(second[j // 2][:, j % 2, :], planes[j][:].indirect(offs_t[:, PIECE // 16 :]), COPY)
             if j == 1:
-                nc.scalar.copy(woven(picked[1][:])[:, :, 0:2, :], by_plane(second[0][:]))
-        nc.vector.tensor_copy(woven(picked[1][:])[:, :, 2:4, :], by_plane(second[1][:]))
+                nc.scalar.copy(woven(rest[:])[:, :, 0:2, :], by_plane(second[0][:]))
+        nc.vector.tensor_copy(woven(rest[:])[:, :, 2:4, :], by_plane(second[1][:]))
 
         warm_codes = sbuf([P, PIECE], U32, "warm_codes")
         warm_scales = sbuf([P, PIECE], U8, "warm_scales")
@@ -104,7 +106,7 @@ def tile_picked_pna_none_e_kernel(
                 out=warm_codes[:, cols].bitcast(FP8X4), scales=warm_scales[:, cols], in_=second[0][:].rearrange("p e n -> p (e n)")
             )
         spare = bank(7, [P, PIECE])
-        nc.tensor.transpose(spare[:, :P], w1_raw[0][:, 0, :P], identity[:])
+        nc.tensor.transpose(spare[:, :P], second[1][:, 1, : 2 * P].bitcast(F32), identity[:])
         for i in range(3):
             nc.tensor.matmul_mx(
                 out=spare[:],
@@ -125,20 +127,8 @@ def tile_picked_pna_none_e_kernel(
                     w1_cols[:, :, :, 2 * u : 2 * u + 2],
                     COPY,
                 )
-        x_q = [None, None]
-        w1_q = [None, None]
-        x_q[0] = quantize(picked[0][:], PIECE, "x0")
-        w1_q[0] = quantize(w1_grouped[0][:].rearrange("p t m j -> p (t m j)"), 2 * P, "w1_0")
-        late_codes = sbuf([P, PIECE], U32, "x1_codes", tag="w1_grouped0")
-        late_scales = sbuf([P, PIECE], U8, "x1_scales")
-        cuts = (0, 256, 384, 512)
-        for lo, hi in zip(cuts, cuts[1:]):
-            nc.vector.quantize_mx(
-                out=late_codes[:, lo:hi].bitcast(FP8X4),
-                scales=late_scales[:, lo:hi],
-                in_=picked[1][:, lo * PACK : hi * PACK],
-            )
-        x_q[1] = (late_codes, late_scales)
+        x_q = [quantize(picked[:], PIECE, "x0", tag="plane3"), quantize(rest[:], PIECE, "x1")]
+        w1_q = [quantize(w1_grouped[u][:].rearrange("p t m j -> p (t m j)"), 2 * P, "w1_%d" % u) for u in range(2)]
 
         blocks = V // P
 
@@ -158,12 +148,11 @@ def tile_picked_pna_none_e_kernel(
                 added[b].append(t)
 
         h = []
-        pair_tags = {(1, 0): "pair0_0", (2, 0): "w1_1_codes"}
         pairs = {}
 
         def plane_of(d, t):
             if (d, t // 2) not in pairs:
-                pairs[(d, t // 2)] = sbuf([P, 2, V], F32, "pair%d_%d" % (d, t // 2), tag=pair_tags.get((d, t // 2)))
+                pairs[(d, t // 2)] = sbuf([P, 2, V], F32, "pair%d_%d" % (d, t // 2))
             return t, pairs[(d, t // 2)][:, t % 2, :]
 
         def gather(plane, d, first, width, on_vector):
@@ -180,14 +169,13 @@ def tile_picked_pna_none_e_kernel(
         def by_row(tile):
             return tile.rearrange("p e (c i) -> p c e i", i=4)
 
-        first_list = [sbuf([P, 2 * V], BF16, "first_list%d" % u) for u in range(2)]
         for t in range(PACK):
             row = sbuf([P, S], F32, "h%d" % t)
             w_codes, w_scales = w1_q[t // 2]
             cols = slice((t % 2) * P, (t % 2 + 1) * P)
-            spans = [(0, 0, PIECE)] + [(1, lo, hi) for lo, hi in zip(cuts, cuts[1:])] if t == 0 else [(1, 0, PIECE), (0, 0, PIECE)]
+            spans = [(s, lo, lo + PIECE // 2) for s in range(2) for lo in (0, PIECE // 2)] if t == 0 else [(0, 0, PIECE), (1, 0, PIECE)]
             for i, (s, lo, hi) in enumerate(spans):
-                acc = bank(((0, 1, 2, 3), (4, 0), (5, 6), (7, 1))[t][i], [P, hi - lo])
+                acc = bank(((0, 1, 2, 3), (4, 5), (6, 7), (0, 1))[t][i], [P, hi - lo])
                 nc.tensor.matmul_mx(
                     out=acc[:],
                     lhsT=w_codes[:, cols].bitcast(FP8X4),
@@ -197,24 +185,34 @@ def tile_picked_pna_none_e_kernel(
                     start=True,
                     stop=True,
                 )
-                if s == 1 and t == 0:
+                if t == 0 and i % 2 == 1:
                     nc.vector.tensor_copy(row[:, s * PIECE + lo : s * PIECE + hi], acc[:])
                 else:
                     nc.scalar.copy(row[:, s * PIECE + lo : s * PIECE + hi], acc[:])
-            if t == 0:
-                w1_q[1] = quantize(w1_grouped[1][:].rearrange("p t m j -> p (t m j)"), 2 * P, "w1_1")
             h.append(row)
             gather(plane_of(0, t), 0, 0, V, True)
-            if t % 2 == 1:
-                nc.gpsimd.tensor_scalar(paired(first_list[t // 2][:]), by_row(pairs[(0, t // 2)][:]), 1.0, 0.0, MULT, ADD)
-        sums = [bank(b, [P, PACK * P]) for b in (2, 3, 0, 4)]
+            if t < 2:
+                gather(plane_of(1, t), 1, 0, V, True)
+        sums = [bank(2 + b, [P, PACK * P]) for b in range(blocks)]
+        for t in (2, 3):
+            gather(plane_of(1, t), 1, 0, V, False)
         for t in range(PACK):
-            add_turned(plane_of(0, t), 0, V)
+            for d in range(2):
+                add_turned(plane_of(d, t), 0, V)
+        early = {}
+        for d, u in ((0, 0), (1, 0), (1, 1), (0, 1)):
+            early[(d, u)] = sbuf([P, 2 * V], BF16, "early%d_%d" % (d, u))
+            if (d, u) == (0, 1):
+                nc.vector.tensor_copy(paired(early[(d, u)][:]), by_row(pairs[(d, u)][:]))
+            else:
+                nc.gpsimd.tensor_scalar(
+                    early[(d, u)][:].rearrange("p (v e) -> p v e", e=2), pairs[(d, u)][:].rearrange("p e v -> p v e"), 1.0, 0.0, MULT, ADD
+                )
 
         out_rows = out.rearrange("(m p) v -> p m v", p=P)
-        accs = {0: [bank(b, [P, HALF]) for b in (7, 1)]}
+        accs = {0: [bank(b, [P, HALF]) for b in (0, 1)]}
         for b in range(2):
-            accs[HALF + b * P] = [bank(((2, 3), (0, 4))[b][m], [P, P]) for m in range(N // P)]
+            accs[HALF + b * P] = [bank(2 + 2 * b + m, [P, P]) for m in range(N // P)]
 
         def fetch(plane, d, first, width, on_vector=False):
             gather(plane, d, first, width, on_vector)
@@ -241,7 +239,7 @@ def tile_picked_pna_none_e_kernel(
             nc.vector.tensor_copy(woven(tile[:]), by_plane(late[:, :, first : first + HALF]))
             return tile
 
-        backs = [bank(b, [P, 2, 2, P]) for b in (5, 6)]
+        backs = [bank(b, [P, 2, 2, P]) for b in (6, 7)]
 
         def turn_back(b):
             mean_t = sbuf([P, 2, P, 2], BF16, "mean_t%d" % b)
@@ -263,44 +261,47 @@ def tile_picked_pna_none_e_kernel(
             second_engine(result[:, 1, :], accs[first][1][:])
             nc.sync.dma_start(out=out_rows[:, :, first : first + width], in_=result[:])
 
-        last = sbuf([P, PACK, V], F32, "last", tag="w1_grouped0")
-        hi3 = sbuf([P, 2, 2 * V], BF16, "hi3")
-        lo3 = sbuf([P, 2, 2 * V], BF16, "lo3")
+        third = sbuf([P, PACK, V], F32, "third", tag="w1_1_codes")
+        last = sbuf([P, PACK, V], F32, "last", tag="x1_codes")
+        hi2 = sbuf([P, 2, 2 * V], BF16, "hi2")
+        lo2 = sbuf([P, 2, 2 * V], BF16, "lo2")
 
-        def three_lists(u):
-            hi2, lo2 = [sbuf([P, 2 * V], BF16, "%s%d" % (name, u)) for name in ("hi2_", "lo2_")]
-            nc.vector.tensor_tensor(paired(hi2[:]), by_row(pairs[(1, u)][:]), by_row(pairs[(2, u)][:]), MAX)
-            nc.vector.tensor_tensor(paired(lo2[:]), by_row(pairs[(1, u)][:]), by_row(pairs[(2, u)][:]), MIN)
-            nc.vector.tensor_tensor(hi3[:, u, :], hi2[:], first_list[u][:], MAX)
-            nc.vector.tensor_tensor(lo3[:, u, :], lo2[:], first_list[u][:], MIN)
-
-        def four_lists(name, three, first, width, op):
-            tile = sbuf([P, width * PACK], BF16, name)
-            at = first % HALF
+        def three_lists(name, two, half, op):
+            tile = sbuf([P, HALF * PACK], BF16, "%s%d" % (name, half))
             nc.vector.tensor_tensor(
                 tile[:].rearrange("p (v u e) -> p v u e", u=2, e=2),
-                three[:, :, 2 * first : 2 * (first + width)].rearrange("p u (v e) -> p v u e", e=2),
-                fourth[first // HALF][:, at * PACK : (at + width) * PACK].rearrange("p (v u e) -> p v u e", u=2, e=2),
+                two[:, :, half * V : (half + 1) * V].rearrange("p u (v e) -> p v u e", e=2),
+                third_r[half][:].rearrange("p (v u e) -> p v u e", u=2, e=2),
                 op,
             )
             return tile
 
-        fetch(plane_of(1, 3), 1, 0, V, on_vector=True)
-        for d, t in ((2, 3), (1, 2), (2, 2)):
-            fetch(plane_of(d, t), d, 0, V)
-        fetch(plane_of(1, 1), 1, 0, V, on_vector=True)
-        for d, t in ((2, 0), (1, 0), (2, 1)):
-            fetch(plane_of(d, t), d, 0, V)
-        three_lists(1)
-        three_lists(0)
+        def four_lists(name, three, first, width, op):
+            tile = sbuf([P, width * PACK], BF16, name)
+            span = slice(first % HALF * PACK, (first % HALF + width) * PACK)
+            nc.vector.tensor_tensor(tile[:], three[first // HALF][:, span], fourth[first // HALF][:, span], op)
+            return tile
+
         fetch((PACK - 1, last[:, PACK - 1, :]), 3, 0, HALF, on_vector=True)
-        for t in range(PACK - 1):
+        for t in range(PACK):
+            fetch((t, third[:, t, :]), 2, 0, V)
+        for t in range(2):
             fetch((t, last[:, t, :]), 3, 0, V)
-        fetch((PACK - 1, last[:, PACK - 1, :]), 3, HALF, HALF)
-        fourth = [rounded(last, 3, half * HALF) for half in range(2)]
+        for t, first in ((2, 0), (2, HALF), (3, HALF)):
+            fetch((t, last[:, t, :]), 3, first, HALF)
+        for u in range(2):
+            nc.vector.tensor_tensor(hi2[:, u, :], early[(0, u)][:], early[(1, u)][:], MAX)
+            nc.vector.tensor_tensor(lo2[:, u, :], early[(0, u)][:], early[(1, u)][:], MIN)
+        third_r = [rounded(third, 2, half * HALF) for half in range(2)]
+        hi3 = [three_lists("hi3_", hi2, 0, MAX)]
+        lo3 = [three_lists("lo3_", lo2, 0, MIN)]
+        hi3.append(three_lists("hi3_", hi2, 1, MAX))
+        fourth = [rounded(last, 3, 0)]
+        lo3.append(three_lists("lo3_", lo2, 1, MIN))
         hi_first = four_lists("hi_first", hi3, 0, HALF, MAX)
         lo_first = four_lists("lo_first", lo3, 0, HALF, MIN)
         out_passes(1, codes_of(1, hi_first, 0, HALF), 0, HALF, True, False)
+        fourth.append(rounded(last, 3, HALF))
         out_passes(2, codes_of(2, lo_first, 0, HALF), 0, HALF, False, False)
         turn_back(0)
         turn_back(1)

@@ -191,23 +191,19 @@ def tile_picked_pna_none_e_kernel(
                     nc.scalar.copy(row[:, s * PIECE + lo : s * PIECE + hi], acc[:])
             h.append(row)
             gather(plane_of(0, t), 0, 0, V, True)
-            if t < 2:
-                gather(plane_of(1, t), 1, 0, V, True)
         sums = [bank(2 + b, [P, PACK * P]) for b in range(blocks)]
-        for t in (2, 3):
-            gather(plane_of(1, t), 1, 0, V, False)
-        for t in range(PACK):
-            for d in range(2):
-                add_turned(plane_of(d, t), 0, V)
+        pairs[(1, 0)] = sbuf([P, 2, V], F32, "pair1_0", tag="x1_scales")
+        pairs[(1, 1)] = sbuf([P, 2, V], F32, "pair1_1", tag="x0_scales")
+        for t in (3, 2, 0, 1):
+            gather(plane_of(1, t), 1, 0, V, t == PACK - 1)
+        for d, t in ((0, 0), (0, 1), (0, 2), (1, 2), (0, 3), (1, 0), (1, 3), (1, 1)):
+            add_turned(plane_of(d, t), 0, V)
         early = {}
-        for d, u in ((0, 0), (1, 0), (1, 1), (0, 1)):
+        for d, u in ((0, 0), (0, 1), (1, 1)):
             early[(d, u)] = sbuf([P, 2 * V], BF16, "early%d_%d" % (d, u))
-            if (d, u) == (0, 1):
-                nc.vector.tensor_copy(paired(early[(d, u)][:]), by_row(pairs[(d, u)][:]))
-            else:
-                nc.gpsimd.tensor_scalar(
-                    early[(d, u)][:].rearrange("p (v e) -> p v e", e=2), pairs[(d, u)][:].rearrange("p e v -> p v e"), 1.0, 0.0, MULT, ADD
-                )
+            nc.gpsimd.tensor_scalar(
+                early[(d, u)][:].rearrange("p (v e) -> p v e", e=2), pairs[(d, u)][:].rearrange("p e v -> p v e"), 1.0, 0.0, MULT, ADD
+            )
 
         out_rows = out.rearrange("(m p) v -> p m v", p=P)
         accs = {0: [bank(b, [P, HALF]) for b in (0, 1)]}
@@ -282,14 +278,17 @@ def tile_picked_pna_none_e_kernel(
             nc.vector.tensor_tensor(tile[:], three[first // HALF][:, span], fourth[first // HALF][:, span], op)
             return tile
 
+        fetch((PACK - 1, third[:, PACK - 1, :]), 2, 0, V, on_vector=True)
         fetch((PACK - 1, last[:, PACK - 1, :]), 3, 0, HALF, on_vector=True)
-        for t in range(PACK):
+        early[(1, 0)] = sbuf([P, 2 * V], BF16, "early1_0", tag="x0_scales")
+        nc.vector.tensor_copy(paired(early[(1, 0)][:]), by_row(pairs[(1, 0)][:]))
+        for t in range(PACK - 1):
             fetch((t, third[:, t, :]), 2, 0, V)
         for t in range(2):
             fetch((t, last[:, t, :]), 3, 0, V)
         for t, first in ((2, 0), (2, HALF), (3, HALF)):
             fetch((t, last[:, t, :]), 3, first, HALF)
-        for u in range(2):
+        for u in (1, 0):
             nc.vector.tensor_tensor(hi2[:, u, :], early[(0, u)][:], early[(1, u)][:], MAX)
             nc.vector.tensor_tensor(lo2[:, u, :], early[(0, u)][:], early[(1, u)][:], MIN)
         third_r = [rounded(third, 2, half * HALF) for half in range(2)]

from contextlib import ExitStack

import concourse.mybir as mybir
from concourse.masks import make_identity

K, T, S, V, H, N = 512, 4096, 1024, 512, 512, 256
FLOPS = 2 * K * H * S + 3 * 2 * H * N * V

F32 = mybir.dt.float32
BF16 = mybir.dt.bfloat16
I32 = mybir.dt.int32
U32 = mybir.dt.uint32
U16 = mybir.dt.uint16
U8 = mybir.dt.uint8
FP8X4 = mybir.dt.float8_e4m3fn_x4
FP4X4 = mybir.dt.float4_e2m1fn_x4
COPY = mybir.ActivationFunctionType.Copy
MAX = mybir.AluOpType.max
MIN = mybir.AluOpType.min
MULT = mybir.AluOpType.mult
ADD = mybir.AluOpType.add

P = 128
PACK = 4
D = 4
PIECE = 512
HALF = V // 2


def tile_picked_pna_none_e_kernel(
    tc, xT, w1, w2_words, w2_scales, w3_words, w3_scales, w4_words, w4_scales, offs, pos1, pos2, pos3, pos4, out
):
    nc = tc.nc
    with ExitStack() as ctx:
        keep = ctx.enter_context(tc.tile_pool(name="keep", bufs=1))
        psum = ctx.enter_context(tc.psum_pool(name="psum", bufs=1))

        def sbuf(shape, dtype, name, tag=None):
            return keep.tile(shape, dtype, name=name, tag=tag or name, align_bytes=64)

        def bank(b, shape):
            return psum.tile(shape, F32, name="bank%d" % b)

        def quantize(values, width, name, tag=None):
            codes = sbuf([P, width], U32, name + "_codes", tag=tag)
            scales = sbuf([P, width], U8, name + "_scales")
            nc.vector.quantize_mx(out=codes[:].bitcast(FP8X4), scales=scales[:], in_=values)
            return codes, scales

        def woven(tile):
            return tile.rearrange("p (c i t) -> p c t i", i=4, t=PACK)

        def by_plane(tile):
            return tile.rearrange("p t (c i) -> p c t i", i=4)

        x_rows = xT.rearrange("(p j) t -> p j t", j=PACK)
        planes = [sbuf([P, T], F32, "plane%d" % j) for j in range(PACK)]
        offs_t = keep.tile([P, S // 16], U16, name="offs")
        nc.sync.dma_start(out=planes[0][:], in_=x_rows[:, 0, :])
        nc.sync.dma_start(offs_t[:], offs)
        for j in range(1, PACK):
            nc.sync.dma_start(out=planes[j][:], in_=x_rows[:, j, :])
        w1_rows = w1.rearrange("(p j) c -> p j c", j=PACK)
        w1_raw = [sbuf([P, PACK, H // 2], F32, "w1_raw%d" % half) for half in range(2)]
        for half in range(2):
            nc.sync.dma_start(out=w1_raw[half][:], in_=w1_rows[:, :, half * H // 2 : (half + 1) * H // 2])
        pos_t = []
        for d, pos in enumerate((pos1, pos2, pos3, pos4)):
            tile = keep.tile([P, V // 16], U16, name="pos%d" % d)
            nc.sync.dma_start(tile[:], pos)
            pos_t.append(tile)
        out_scales = sbuf([P, 3 * N], U8, "out_scales")
        nc.gpsimd.memset(out_scales[:].bitcast(I32), 0)
        out_words = []
        for a, words in enumerate((w2_words, w3_words, w4_words)):
            tile = sbuf([P, 2 * N], U8, "out_words%d" % a)
            nc.sync.dma_start(out=tile[:].bitcast(I32), in_=words[0].bitcast(I32))
            out_words.append(tile)
        for a, scales in enumerate((w2_scales, w3_scales, w4_scales)):
            for q in range(4):
                nc.sync.dma_start(
                    out=out_scales[32 * q : 32 * q + 4, a * N : (a + 1) * N].bitcast(I32),
                    in_=scales[0, 4 * q : 4 * q + 4, :].bitcast(I32),
                )
        identity = sbuf([P, P], F32, "identity")
        make_identity(nc, identity[:])

        picked = sbuf([P, PIECE * PACK], BF16, "picked")
        rest = sbuf([P, PIECE * PACK], BF16, "rest")
        second = [sbuf([P, 2, PIECE], BF16, "second%d" % u) for u in range(2)]

        for j in range(PACK):
            nc.vector.tensor_copy(
                picked[:].rearrange("p (n j) -> p n j", j=PACK)[:, :, j], planes[j][:].indirect(offs_t[:, : PIECE // 16])
            )
            nc.scalar.activation(second[j // 2][:, j % 2, :], planes[j][:].indirect(offs_t[:, PIECE // 16 :]), COPY)
            if j == 1:
                nc.scalar.copy(woven(rest[:])[:, :, 0:2, :], by_plane(second[0][:]))
        nc.vector.tensor_copy(woven(rest[:])[:, :, 2:4, :], by_plane(second[1][:]))

        warm_codes = sbuf([P, PIECE], U32, "warm_codes")
        warm_scales = sbuf([P, PIECE], U8, "warm_scales")
        for i in range(2):
            cols = slice(i * PIECE // 2, (i + 1) * PIECE // 2)
            nc.vector.quantize_mx(
                out=warm_codes[:, cols].bitcast(FP8X4), scales=warm_scales[:, cols], in_=second[0][:].rearrange("p e n -> p (e n)")
            )
        spare = bank(7, [P, PIECE])
        nc.tensor.transpose(spare[:, :P], second[1][:, 1, : 2 * P].bitcast(F32), identity[:])
        for i in range(3):
            nc.tensor.matmul_mx(
                out=spare[:],
                lhsT=warm_codes[:, :P].bitcast(FP8X4),
                lhsT_scale=warm_scales[:, :P],
                rhs=warm_codes[:].bitcast(FP8X4),
                rhs_scale=warm_scales[:],
                start=True,
                stop=True,
            )

        w1_grouped = [sbuf([P, 2, P, PACK], BF16, "w1_grouped%d" % u) for u in range(2)]
        for half in range(2):
            w1_cols = w1_raw[half][:].rearrange("p j (m t) -> p m j t", t=PACK)
            for u in range(2):
                nc.scalar.activation(
                    w1_grouped[u][:, :, half * P // 2 : (half + 1) * P // 2, :].rearrange("p t m j -> p m j t"),
                    w1_cols[:, :, :, 2 * u : 2 * u + 2],
                    COPY,
                )
        x_q = [quantize(picked[:], PIECE, "x0", tag="plane3"), quantize(rest[:], PIECE, "x1")]
        w1_q = [quantize(w1_grouped[u][:].rearrange("p t m j -> p (t m j)"), 2 * P, "w1_%d" % u) for u in range(2)]

        blocks = V // P

        added = [[] for b in range(blocks)]

        def add_turned(plane, first, width):
            t, values = plane
            for b in range(first // P, (first + width) // P):
                nc.tensor.matmul(
                    sums[b][:, t * P : (t + 1) * P],
                    values[:, b * P : (b + 1) * P],
                    identity[:],
                    start=(len(added[b]) == 0),
                    stop=(len(added[b]) == D * PACK - 1),
                    is_transpose=True,
                )
                added[b].append(t)

        h = []
        pairs = {}

        def plane_of(d, t):
            if (d, t // 2) not in pairs:
                pairs[(d, t // 2)] = sbuf([P, 2, V], F32, "pair%d_%d" % (d, t // 2))
            return t, pairs[(d, t // 2)][:, t % 2, :]

        def gather(plane, d, first, width, on_vector):
            t, values = plane
            window = h[t][:].indirect(pos_t[d][:, first // 16 : (first + width) // 16])
            if on_vector:
                nc.vector.tensor_copy(values[:, first : first + width], window)
            else:
                nc.scalar.activation(values[:, first : first + width], window, COPY)

        def paired(tile):
            return tile.rearrange("p (c i e) -> p c e i", i=4, e=2)

        def by_row(tile):
            return tile.rearrange("p e (c i) -> p c e i", i=4)

        for t in range(PACK):
            row = sbuf([P, S], F32, "h%d" % t)
            w_codes, w_scales = w1_q[t // 2]
            cols = slice((t % 2) * P, (t % 2 + 1) * P)
            spans = [(s, lo, lo + PIECE // 2) for s in range(2) for lo in (0, PIECE // 2)] if t == 0 else [(0, 0, PIECE), (1, 0, PIECE)]
            for i, (s, lo, hi) in enumerate(spans):
                acc = bank(((0, 1, 2, 3), (4, 5), (6, 7), (0, 1))[t][i], [P, hi - lo])
                nc.tensor.matmul_mx(
                    out=acc[:],
                    lhsT=w_codes[:, cols].bitcast(FP8X4),
                    lhsT_scale=w_scales[:, cols],
                    rhs=x_q[s][0][:, lo:hi].bitcast(FP8X4),
                    rhs_scale=x_q[s][1][:, lo:hi],
                    start=True,
                    stop=True,
                )
                if t == 0 and i % 2 == 1:
                    nc.vector.tensor_copy(row[:, s * PIECE + lo : s * PIECE + hi], acc[:])
                else:
                    nc.scalar.copy(row[:, s * PIECE + lo : s * PIECE + hi], acc[:])
            h.append(row)
            gather(plane_of(0, t), 0, 0, V, True)
        sums = [bank(2 + b, [P, PACK * P]) for b in range(blocks)]
        pairs[(1, 0)] = sbuf([P, 2, V], F32, "pair1_0", tag="x1_scales")
        pairs[(1, 1)] = sbuf([P, 2, V], F32, "pair1_1", tag="x0_scales")
        for t in (3, 2, 0, 1):
            gather(plane_of(1, t), 1, 0, V, t == PACK - 1)
        for d, t in ((0, 0), (0, 1), (0, 2), (1, 2), (0, 3), (1, 0), (1, 3), (1, 1)):
            add_turned(plane_of(d, t), 0, V)
        early = {}
        for d, u in ((0, 0), (0, 1), (1, 1)):
            early[(d, u)] = sbuf([P, 2 * V], BF16, "early%d_%d" % (d, u))
            nc.gpsimd.tensor_scalar(
                early[(d, u)][:].rearrange("p (v e) -> p v e", e=2), pairs[(d, u)][:].rearrange("p e v -> p v e"), 1.0, 0.0, MULT, ADD
            )

        out_rows = out.rearrange("(m p) v -> p m v", p=P)
        accs = {0: [bank(b, [P, HALF]) for b in (0, 1)]}
        for b in range(2):
            accs[HALF + b * P] = [bank(2 + 2 * b + m, [P, P]) for m in range(N // P)]

        def fetch(plane, d, first, width, on_vector=False):
            gather(plane, d, first, width, on_vector)
            add_turned(plane, first, width)

        def codes_of(a, values, first, width, tag=None):
            return quantize(values[:], width, "z%d_%d" % (a, first), tag=tag)

        def out_passes(a, quantized, first, width, start, stop, skip=0):
            codes, scales = quantized
            for m in range(N // P):
                nc.tensor.matmul_mx(
                    out=accs[first][m][:],
                    lhsT=out_words[a][:, 2 * P * m : 2 * P * (m + 1)].bitcast(FP4X4),
                    lhsT_scale=out_scales[:, a * N + m * P : a * N + (m + 1) * P],
                    rhs=codes[:, skip : skip + width].bitcast(FP8X4),
                    rhs_scale=scales[:, skip : skip + width],
                    start=start,
                    stop=stop,
                )

        def rounded(late, d, first):
            tile = sbuf([P, HALF * PACK], BF16, "rounded%d_%d" % (d, first))
            nc.vector.tensor_copy(woven(tile[:]), by_plane(late[:, :, first : first + HALF]))
            return tile

        backs = [bank(b, [P, 2, 2, P]) for b in (6, 7)]

        def turn_back(b):
            mean_t = sbuf([P, 2, P, 2], BF16, "mean_t%d" % b)
            nc.scalar.activation(mean_t[:], sums[b][:].rearrange("v (u e p) -> v u p e", u=2, e=2), COPY, scale=0.25)
            words = mean_t[:].rearrange("v u p e -> v (u p e)").bitcast(F32)
            for u in range(2):
                nc.tensor.transpose(backs[b // 2][:, b % 2, u, :], words[:, u * P : (u + 1) * P], identity[:])

        def mean_of(half):
            mean = sbuf([P, HALF * PACK], BF16, "mean%d" % half)
            nc.scalar.copy(
                mean[:].bitcast(F32).rearrange("p (i v u) -> p i v u", v=P, u=2), backs[half][:].rearrange("p i u v -> p i v u")
            )
            return mean

        def store(first, width, second_engine):
            result = sbuf([P, N // P, width], F32, "result%d" % first)
            nc.scalar.copy(result[:, 0, :], accs[first][0][:])
            second_engine(result[:, 1, :], accs[first][1][:])
            nc.sync.dma_start(out=out_rows[:, :, first : first + width], in_=result[:])

        third = sbuf([P, PACK, V], F32, "third", tag="w1_1_codes")
        last = sbuf([P, PACK, V], F32, "last", tag="x1_codes")
        hi2 = sbuf([P, 2, 2 * V], BF16, "hi2")
        lo2 = sbuf([P, 2, 2 * V], BF16, "lo2")

        def three_lists(name, two, half, op):
            tile = sbuf([P, HALF * PACK], BF16, "%s%d" % (name, half))
            nc.vector.tensor_tensor(
                tile[:].rearrange("p (v u e) -> p v u e", u=2, e=2),
                two[:, :, half * V : (half + 1) * V].rearrange("p u (v e) -> p v u e", e=2),
                third_r[half][:].rearrange("p (v u e) -> p v u e", u=2, e=2),
                op,
            )
            return tile

        def four_lists(name, three, first, width, op):
            tile = sbuf([P, width * PACK], BF16, name)
            span = slice(first % HALF * PACK, (first % HALF + width) * PACK)
            nc.vector.tensor_tensor(tile[:], three[first // HALF][:, span], fourth[first // HALF][:, span], op)
            return tile

        fetch((PACK - 1, third[:, PACK - 1, :]), 2, 0, V, on_vector=True)
        fetch((PACK - 1, last[:, PACK - 1, :]), 3, 0, HALF, on_vector=True)
        early[(1, 0)] = sbuf([P, 2 * V], BF16, "early1_0", tag="x0_scales")
        nc.vector.tensor_copy(paired(early[(1, 0)][:]), by_row(pairs[(1, 0)][:]))
        for t in range(PACK - 1):
            fetch((t, third[:, t, :]), 2, 0, V)
        for t in range(2):
            fetch((t, last[:, t, :]), 3, 0, V)
        for t, first in ((2, 0), (2, HALF), (3, HALF)):
            fetch((t, last[:, t, :]), 3, first, HALF)
        for u in (1, 0):
            nc.vector.tensor_tensor(hi2[:, u, :], early[(0, u)][:], early[(1, u)][:], MAX)
            nc.vector.tensor_tensor(lo2[:, u, :], early[(0, u)][:], early[(1, u)][:], MIN)
        third_r = [rounded(third, 2, half * HALF) for half in range(2)]
        hi3 = [three_lists("hi3_", hi2, 0, MAX)]
        lo3 = [three_lists("lo3_", lo2, 0, MIN)]
        hi3.append(three_lists("hi3_", hi2, 1, MAX))
        fourth = [rounded(last, 3, 0)]
        lo3.append(three_lists("lo3_", lo2, 1, MIN))
        hi_first = four_lists("hi_first", hi3, 0, HALF, MAX)
        lo_first = four_lists("lo_first", lo3, 0, HALF, MIN)
        out_passes(1, codes_of(1, hi_first, 0, HALF), 0, HALF, True, False)
        fourth.append(rounded(last, 3, HALF))
        out_passes(2, codes_of(2, lo_first, 0, HALF), 0, HALF, False, False)
        turn_back(0)
        turn_back(1)
        first_mean = mean_of(0)
        turn_back(2)
        turn_back(3)
        last_mean = mean_of(1)
        hi = four_lists("hi_last", hi3, HALF, HALF, MAX)
        out_passes(0, codes_of(0, first_mean, 0, HALF), 0, HALF, False, True)
        store(0, HALF, nc.scalar.copy)

        def last_smallest(b):
            return four_lists("lo_last%d" % b, lo3, HALF + b * P, P, MIN)

        lows = [last_smallest(0)]
        hi_q = codes_of(1, hi, HALF, HALF)
        for b in range(2):
            out_passes(1, hi_q, HALF + b * P, P, True, False, skip=b * P)
        lows.append(last_smallest(1))
        mean_q = codes_of(0, last_mean, HALF, HALF)
        for b in range(2):
            out_passes(0, mean_q, HALF + b * P, P, False, False, skip=b * P)
        for b in range(2):
            out_passes(2, codes_of(2, lows[b], HALF + b * P, P), HALF + b * P, P, False, True)
        store(HALF, P, nc.vector.tensor_copy)
        store(HALF + P, P, nc.vector.tensor_copy)
